import numpy as np
import ml_dtypes


def mxq(x, axis, fmt="e4m3"):
    dtype, down = {"e4m3": (ml_dtypes.float8_e4m3fn, 7), "e5m2": (ml_dtypes.float8_e5m2, 14)}[fmt]
    v = np.moveaxis(np.asarray(x, np.float32).astype(ml_dtypes.bfloat16).astype(np.float64), axis, -1)
    blocks = v.reshape(v.shape[:-1] + (-1, 32))
    amax = np.abs(blocks).max(-1, keepdims=True)
    byte = np.maximum(np.where(amax > 0, np.frexp(amax)[1] - 1 + 127, 0) - down, 1)
    scale = np.exp2(byte - 127.0)
    codes = (blocks / scale).astype(np.float32).astype(dtype).astype(np.float64)
    return np.moveaxis((codes * scale).reshape(v.shape), -1, axis)


WIDE = False


def mx_kscale(k):
    if not WIDE:
        return np.ones(k)
    levels = np.array([10, -10, 5, -5, 0])
    if k % 512:
        return np.exp2(np.random.permutation(np.resize(levels, k // 32))).repeat(32)
    a = np.empty((k // 512, 16))
    for p in range(k // 512):
        a[p, :8] = np.random.permutation(np.resize(levels, 8))
        for g in range(8):
            far = levels[np.abs(levels - a[p, g]) >= 10]
            a[p, g + 8] = far[np.random.randint(len(far))]
    return np.exp2(a.ravel()).repeat(32)


BF16 = ml_dtypes.bfloat16


def bf(x):
    return np.asarray(x, np.float32).astype(BF16)


def f64(x):
    return np.asarray(x).astype(np.float64)


E2M1 = np.array([0.0, 0.5, 1.0, 1.5, 2.0, 3.0, 4.0, 6.0, -0.0, -0.5, -1.0, -1.5, -2.0, -3.0, -4.0, -6.0])


def pack_weight(w, fmt):
    k, n = w.shape
    w = f64(bf(w)).reshape(k // 32, 32, n)
    amax = np.abs(w).max(1)
    if fmt == "e4m3":
        byte = np.frexp(amax)[1] - 1 + 127 - 7
    else:
        mant, ex = np.frexp(amax / 6.0)
        byte = np.where(mant > 0.5, ex, ex - 1) + 127
    byte = np.clip(np.where(amax > 0, byte, 1), 1, 254)
    scaled = (w * np.exp2(127.0 - byte)[:, None, :]).reshape(k, n).astype(np.float32)
    by_word = np.ascontiguousarray(scaled.reshape(k // 512, 128, 4, n).transpose(0, 1, 3, 2))
    if fmt == "e4m3":
        words = by_word.astype(ml_dtypes.float8_e4m3fn).view(np.uint8)
    else:
        c = by_word.astype(ml_dtypes.float4_e2m1fn).view(np.uint8) & 0xF
        words = c[..., 0::2] | (c[..., 1::2] << 4)
    return np.ascontiguousarray(words), np.ascontiguousarray(byte.astype(np.uint8).reshape(k // 512, 16, n))


def unpack_weight(words, scales, fmt):
    g, p, n, _ = words.shape
    if fmt == "e4m3":
        vals = np.ascontiguousarray(words).view(ml_dtypes.float8_e4m3fn).astype(np.float64)
    else:
        nib = np.empty((g, p, n, 4), np.uint8)
        nib[..., 0::2] = words & 0xF
        nib[..., 1::2] = words >> 4
        vals = E2M1[nib]
    vals = vals * np.repeat(np.exp2(scales.astype(np.float64) - 127.0), 8, axis=1)[..., None]
    return vals.transpose(0, 1, 3, 2).reshape(g * 512, n)

E4M3FN = np.array([(-1.0 if i & 128 else 1.0) * ((1.0 + (i & 7) / 8.0) * 2.0 ** (((i >> 3) & 15) - 7) if i & 120 else (i & 7) * 2.0 ** -9) for i in range(256)])


def e4m3fn_bytes(y):
    return np.clip(np.asarray(y, np.float64), -448.0, 448.0).astype(np.float32).astype(ml_dtypes.float8_e4m3fn).view(np.uint8)


def e4m3fn_values(b):
    return E4M3FN[b]


B, S, M, D = 2, 512, 1024, 512


def joint_softmax(a, e):
    mx = np.maximum(a.max(-1, keepdims=True), e.max(-1, keepdims=True))
    ea = np.exp(a - mx)
    ee = np.exp(e - mx)
    z = ea.sum(-1, keepdims=True) + ee.sum(-1, keepdims=True)
    return ea / z, ee / z


def draw0():
    s, cs, cm = mx_kscale(D), mx_kscale(S), mx_kscale(M)
    q = bf(np.random.standard_normal((B, S, D)) * 1.5 * s)
    k = bf(np.random.standard_normal((B, S, D)) / s)
    mk_words, mk_scales = pack_weight((np.random.standard_normal((M, D)) / s).T, "e4m3")
    v = bf(np.random.standard_normal((B, S, D)) * 2.0 / cs[:, None])
    mv_words, mv_scales = pack_weight(np.random.standard_normal((M, D)) * 2.0 / cm[:, None], "e4m3")
    return {
        "q": q,
        "k": k,
        "mk_words": mk_words,
        "mk_scales": mk_scales,
        "v": v,
        "mv_words": mv_words,
        "mv_scales": mv_scales,
        "t": bf(np.random.standard_normal(S) * 2.0 * cs),
        "u": bf(np.random.standard_normal(M) * 2.0 * cm),
    }


def core(q, k, mk_words, mk_scales, v, mv_words, mv_scales, t, u):
    scale = np.sqrt(D)
    qq = mxq(f64(q), 2, "e4m3")
    a = (qq @ mxq(f64(k).transpose(0, 2, 1), 1, "e4m3")) / scale
    e = (qq @ unpack_weight(mk_words, mk_scales, "e4m3")) / scale
    p, r = joint_softmax(a, e)
    pg = p * f64(t)[None, None, :]
    rg = r * f64(u)[None, None, :]
    return (mxq(pg, 2, "e4m3") @ mxq(f64(v), 1, "e4m3")) + (mxq(rg, 2, "e4m3") @ unpack_weight(mv_words, mv_scales, "e4m3"))


def setup_inputs():
    drawn = draw0()
    full = np.asarray(drawn['v']).astype(np.float64)
    scale = (np.abs(full).reshape(2, 512, 4, 128).max(axis=(3,)) / 448.0).astype(np.float32)
    given = {}
    for key, value in drawn.items():
        if key == 'v':
            given['v_bytes'] = e4m3fn_bytes(full / np.repeat(scale.astype(np.float64), 128, axis=2))
            given['v_scale'] = scale
        else:
            given[key] = value
    return given


def reference(q, k, mk_words, mk_scales, v_bytes, v_scale, mv_words, mv_scales, t, u):
    return core(q, k, mk_words, mk_scales, e4m3fn_values(v_bytes) * np.repeat(v_scale.astype(np.float64), 128, axis=2), mv_words, mv_scales, t, u)

@@ -1,0 +1,456 @@
+import math
+from contextlib import ExitStack
+
+import concourse.mybir as mybir
+from concourse.masks import make_identity
+
+B, S, M, D = 2, 512, 1024, 512
+FLOPS = 2 * 2 * B * S * (S + M) * D
+
+F32 = mybir.dt.float32
+BF16 = mybir.dt.bfloat16
+I32 = mybir.dt.int32
+U32 = mybir.dt.uint32
+U8 = mybir.dt.uint8
+FP8 = mybir.dt.float8_e4m3fn
+FP8X4 = mybir.dt.float8_e4m3fn_x4
+ALU = mybir.AluOpType
+ACT = mybir.ActivationFunctionType
+AX = mybir.AxisListType
+
+P = 128
+W = S + M
+NT = B * S // P
+TPB = S // P
+CHUNKS = (1, 2, 0)
+SCALE = 1.0 / math.sqrt(D)
+
+
+def tile_persistentmemoryallattentionsignedgains_d1p_kernel(
+    tc, q, k, mk_words, mk_scales, v_bytes, v_scale, mv_words, mv_scales, t, u, out
+):
+    nc = tc.nc
+    with ExitStack() as ctx:
+        const = ctx.enter_context(tc.tile_pool(name="const", bufs=1))
+        work = ctx.enter_context(tc.tile_pool(name="work", bufs=4))
+        results = ctx.enter_context(tc.tile_pool(name="results", bufs=6))
+        small = ctx.enter_context(tc.tile_pool(name="small", bufs=6))
+        ps_score = ctx.enter_context(tc.psum_pool(name="ps_score", bufs=4))
+        ps_turn = ctx.enter_context(tc.psum_pool(name="ps_turn", bufs=3))
+        ps_out = ctx.enter_context(tc.psum_pool(name="ps_out", bufs=1))
+        ctx.enter_context(tc.manual_schedule())
+
+        mk_plane = const.tile([P, M], U8, align_bytes=64, name="mk_plane")
+        mv_plane = const.tile([P, D], U8, align_bytes=64, name="mv_plane")
+        nc.vector.memset(mk_plane[:].bitcast(I32), 0)
+        nc.vector.memset(mv_plane[:].bitcast(I32), 0)
+        warm = const.tile([P, 1], F32, name="warm")
+        nc.vector.memset(warm[:], 0.0)
+        ident = const.tile([P, P], F32, name="ident")
+        make_identity(nc, ident[:])
+
+        q_raw = [const.tile([P, TPB, D], BF16, name="q_raw%d" % b) for b in range(B)]
+        k_raw = [const.tile([P, TPB, D], BF16, name="k_raw%d" % b) for b in range(B)]
+        v_raw = [const.tile([P, 4 * D], U8, name="v_raw%d" % b) for b in range(B)]
+        mk_codes = const.tile([P, M], I32, align_bytes=64, name="mk_codes")
+        mv_codes = const.tile([P, 2, D], I32, align_bytes=64, name="mv_codes")
+        v_sc = const.tile([P, B, 16], F32, name="v_sc")
+        gains = const.tile([P, W], BF16, name="gains")
+
+        def load_rows(dst, src, lo, hi):
+            nc.sync.dma_start(out=dst[:, lo:hi, :], in_=src.rearrange("(r p) d -> p r d", p=P)[:, lo:hi, :])
+
+        load_rows(q_raw[0], q[0], 0, 1)
+        for h in range(2):
+            nc.sync.dma_start(
+                out=mk_codes[:, h * 512 : (h + 1) * 512],
+                in_=mk_words[0, :, h * 512 : (h + 1) * 512, :].rearrange("p n t -> p (n t)").bitcast(I32),
+            )
+        for quad in range(4):
+            nc.scalar.dma_start(
+                out=mk_plane[32 * quad : 32 * quad + 4, :].bitcast(I32),
+                in_=mk_scales[0, 4 * quad : 4 * quad + 4, :].bitcast(I32),
+            )
+        nc.scalar.activation(out=warm[:], in_=warm[:], func=ACT.Exp)
+        load_rows(k_raw[0], k[0], 0, 2)
+        load_rows(k_raw[0], k[0], 2, 4)
+        load_rows(q_raw[0], q[0], 1, 4)
+        nc.sync.dma_start(out=v_sc[:], in_=v_scale.rearrange("b (p t) c -> p b (t c)", t=4))
+        nc.sync.dma_start(out=v_raw[0][:], in_=v_bytes[0].rearrange("(p t) n -> p (t n)", t=4))
+        nc.sync.dma_start(out=gains[:, 0:S], in_=t.partition_broadcast(P))
+        nc.sync.dma_start(out=gains[:, S:W], in_=u.partition_broadcast(P))
+        load_rows(k_raw[1], k[1], 0, 4)
+        for g in range(2):
+            nc.sync.dma_start(out=mv_codes[:, g, :], in_=mv_words[g].rearrange("p n t -> p (n t)").bitcast(I32))
+        for g in range(2):
+            for quad in range(4):
+                nc.sync.dma_start(
+                    out=mv_plane[32 * quad + 4 * g : 32 * quad + 4 * g + 4, :].bitcast(I32),
+                    in_=mv_scales[g, 4 * quad : 4 * quad + 4, :].bitcast(I32),
+                )
+        load_rows(q_raw[1], q[1], 0, 4)
+        nc.sync.dma_start(out=v_raw[1][:], in_=v_bytes[1].rearrange("(p t) n -> p (t n)", t=4))
+
+        q_codes = [const.tile([P, S], U32, align_bytes=64, name="q_codes%d" % b) for b in range(B)]
+        q_plane = [const.tile([P, S], U8, align_bytes=64, name="q_plane%d" % b) for b in range(B)]
+        k_codes = [const.tile([P, S], U32, align_bytes=64, name="k_codes%d" % b) for b in range(B)]
+        k_plane = [const.tile([P, S], U8, align_bytes=64, name="k_plane%d" % b) for b in range(B)]
+        v_codes = [const.tile([P, D], U32, align_bytes=64, name="v_codes%d" % b) for b in range(B)]
+        v_plane = [const.tile([P, D], U8, align_bytes=64, name="v_plane%d" % b) for b in range(B)]
+        q_grp = [const.tile([P, S, 4], BF16, align_bytes=64, name="q_grp%d" % b) for b in range(B)]
+        k_grp = [const.tile([P, S, 4], BF16, align_bytes=64, name="k_grp%d" % b) for b in range(B)]
+        v_wide = [const.tile([P, 4, D], BF16, align_bytes=64, name="v_wide%d" % b) for b in range(B)]
+        v_grp = [const.tile([P, D, 4], BF16, align_bytes=64, name="v_grp%d" % b) for b in range(B)]
+
+        def copy_on(engine, dst, src):
+            if engine is nc.scalar:
+                nc.scalar.copy(out=dst, in_=src)
+            else:
+                nc.vector.tensor_copy(out=dst, in_=src)
+
+        def turn_rows(raw, grp, r0, n, engine):
+            bank = ps_turn.tile([P, n, 2, P], F32, name="bank")
+            words = raw[:].rearrange("p r d -> p (r d)").bitcast(F32)
+            half = D // 2
+            for a in range(n):
+                for e in range(2):
+                    lo = (r0 + a) * half + e
+                    nc.tensor.transpose(bank[:, a, e, :], words[:, lo : (r0 + a + 1) * half : 2], ident[:])
+            dst = grp[:, r0 * P : (r0 + n) * P, :].rearrange("p n f -> p (n f)").bitcast(F32)
+            copy_on(
+                engine,
+                dst.rearrange("p (a n e) -> p a n e", a=n, e=2),
+                bank[:].rearrange("p a e n -> p a n e"),
+            )
+
+        def quantize(codes, plane, grp, lo, hi):
+            nc.vector.quantize_mx(
+                out=codes[:, lo:hi].bitcast(FP8X4),
+                scales=plane[:, lo:hi],
+                in_=grp[:, lo:hi, :].rearrange("p n f -> p (n f)"),
+            )
+
+        def widen_v(b, c, engine):
+            for f in range(4):
+                cols = slice(f * D + c * P, f * D + (c + 1) * P)
+                scale = v_sc[:, b, 4 * f + c : 4 * f + c + 1]
+                dst = v_wide[b][:, f, c * P : (c + 1) * P]
+                if engine is nc.scalar:
+                    nc.scalar.activation(out=dst, in_=v_raw[b][:, cols].bitcast(FP8), func=ACT.Copy, scale=scale)
+                else:
+                    nc.vector.tensor_scalar(
+                        out=dst, in0=v_raw[b][:, cols].bitcast(FP8), scalar1=scale, scalar2=None, op0=ALU.mult
+                    )
+
+        def interleave_v(b, h, engine):
+            cols = slice(h * D // 2, (h + 1) * D // 2)
+            dst, src = v_grp[b][:, cols, :], v_wide[b][:, :, cols].rearrange("p f n -> p n f")
+            if engine is nc.gpsimd:
+                nc.gpsimd.tensor_scalar(out=dst, in0=src, scalar1=1.0, scalar2=0.0, op0=ALU.mult, op1=ALU.add)
+            else:
+                copy_on(engine, dst, src)
+
+        LAST = NT - 1
+        SPLIT = (0, LAST)
+        banks, m3, nm, ex, z3, zs, fac, gained, probs, turned, grouped, pq = ({} for unused in range(12))
+
+        def score(i, c):
+            b, r = divmod(i, TPB)
+            sc = ps_score.tile([P, 512], F32, name="sc")
+            banks[i, c] = sc
+            if c == 0:
+                rhs, rhs_scale = k_codes[b][:], k_plane[b][:]
+            else:
+                cols = slice((c - 1) * 512, c * 512)
+                rhs, rhs_scale = mk_codes[:, cols], mk_plane[:, cols]
+            nc.tensor.matmul_mx(
+                out=sc[:],
+                lhsT=q_codes[b][:, r * P : (r + 1) * P].bitcast(FP8X4),
+                lhsT_scale=q_plane[b][:, r * P : (r + 1) * P],
+                rhs=rhs.bitcast(FP8X4),
+                rhs_scale=rhs_scale,
+                start=True,
+                stop=True,
+            )
+
+        def row_max(i, c):
+            if i not in m3:
+                m3[i] = small.tile([P, 3], F32, name="m3_t")
+                nm[i] = small.tile([P, 3], F32, name="nm_t")
+            nc.vector.tensor_reduce(out=m3[i][:, c : c + 1], in_=banks[i, c][:], axis=AX.X, op=ALU.max)
+
+        def own_shift(i, c):
+            nc.vector.tensor_scalar(
+                out=nm[i][:, c : c + 1], in0=m3[i][:, c : c + 1], scalar1=-SCALE, scalar2=None, op0=ALU.mult
+            )
+
+        def join_shift(i, src):
+            j = small.tile([P, 1], F32, name="join")
+            scratch = small.tile([P, 3], F32, name="scratch")
+            nc.vector.tensor_scalar(
+                out=scratch[:], in0=src[:], scalar1=(1.0 if i in SPLIT else -SCALE), scalar2=None, op0=ALU.mult, op1=ALU.min, accum_out=j[:]
+            )
+            return j
+
+        def exponentials(i, c, bias):
+            if i not in ex:
+                ex[i] = work.tile([P, W], F32, name="ex_t")
+                z3[i] = small.tile([P, 3], F32, name="z3_t")
+            nc.scalar.activation(
+                out=ex[i][:, c * 512 : (c + 1) * 512],
+                in_=banks[i, c][:],
+                func=ACT.Exp,
+                bias=bias,
+                scale=SCALE,
+                accum_out=z3[i][:, c : c + 1],
+            )
+
+        def z_join(i):
+            j = join_shift(i, nm[i])
+            fac[i] = small.tile([P, 3], F32, name="w3_t")
+            nc.scalar.activation(out=fac[i][:], in_=nm[i][:], func=ACT.Exp, bias=j[:], scale=-1.0)
+
+        def z_weigh(i):
+            zw = small.tile([P, 3], F32, name="zw_t")
+            nc.vector.tensor_tensor(out=zw[:], in0=z3[i][:], in1=fac[i][:], op=ALU.mult)
+            z3[i] = zw
+
+        def z_sum(i):
+            zs[i] = small.tile([P, 1], F32, name="zs_t")
+            nc.vector.tensor_reduce(out=zs[i][:], in_=z3[i][:], axis=AX.X, op=ALU.add)
+
+        def z_inv(i):
+            inv = small.tile([P, 1], F32, name="inv")
+            nc.vector.reciprocal(out=inv[:], in_=zs[i][:])
+            zs[i] = inv
+
+        def z_factors(i):
+            if i in SPLIT:
+                f3 = small.tile([P, 3], F32, name="f3_t")
+                nc.vector.tensor_scalar(out=f3[:], in0=fac[i][:], scalar1=zs[i][:], scalar2=None, op0=ALU.mult)
+                fac[i] = [f3[:, c : c + 1] for c in range(3)]
+            else:
+                fac[i] = [zs[i][:]] * 3
+
+        def probs_tile(i):
+            if i not in probs:
+                probs[i] = work.tile([P, W], BF16, align_bytes=64, name="pg")
+
+        def gain_first(i, c):
+            e_g = work.tile([P, 512], F32, name="e_g")
+            cols = slice(c * 512, (c + 1) * 512)
+            nc.gpsimd.tensor_tensor(out=e_g[:], in0=ex[i][:, cols], in1=gains[:, cols], op=ALU.mult)
+            gained[i] = e_g
+
+        def factor_last(i, c):
+            probs_tile(i)
+            nc.scalar.activation(
+                out=probs[i][:, c * 512 : (c + 1) * 512], in_=gained[i][:], func=ACT.Copy, scale=fac[i][c]
+            )
+
+        def normalise(i, c):
+            probs_tile(i)
+            cols = slice(c * 512, (c + 1) * 512)
+            nc.vector.scalar_tensor_tensor(
+                out=probs[i][:, cols], in0=ex[i][:, cols], scalar=fac[i][c], in1=gains[:, cols], op0=ALU.mult, op1=ALU.mult
+            )
+
+        def turn_probs(i, lo, hi):
+            words = probs[i][:].bitcast(F32)
+            bank = ps_turn.tile([P, hi - lo, 2, P], F32, name="bank")
+            turned[i, lo] = bank
+            for g in range(lo, hi):
+                for e in range(2):
+                    nc.tensor.transpose(bank[:, g - lo, e, :], words[:, 256 * g + e : 256 * (g + 1) : 2], ident[:])
+
+        def copy_probs(i, lo, hi, engine):
+            if i not in grouped:
+                grouped[i] = work.tile([P, 3 * P, 4], BF16, align_bytes=64, name="pg_grp")
+            dst = grouped[i][:].rearrange("p n f -> p (n f)").bitcast(F32).rearrange("p (a n e) -> p a n e", a=3, e=2)
+            copy_on(engine, dst[:, lo:hi], turned[i, lo][:].rearrange("p a e n -> p a n e"))
+
+        def quantize_probs(i, lo, hi):
+            if i not in pq:
+                codes = work.tile([P, 3 * P], U32, align_bytes=64, name="p_codes")
+                plane = work.tile([P, 3 * P], U8, align_bytes=64, name="p_plane")
+                pq[i] = (codes, plane)
+            codes, plane = pq[i]
+            quantize(codes, plane, grouped[i], lo * P, hi * P)
+
+        def mix(i, o, g, first, last, lo=0, hi=D):
+            b = i // TPB
+            codes, plane = pq[i]
+            if g == 0:
+                rhs, rhs_scale = v_codes[b][:, lo:hi], v_plane[b][:, lo:hi]
+            elif g == 1:
+                rhs, rhs_scale = mv_codes[:, 0, lo:hi], mv_plane[:, lo:hi]
+            else:
+                rhs, rhs_scale = mv_codes[:, 1, lo:hi], mv_plane[4:P, lo:hi]
+            nc.tensor.matmul_mx(
+                out=o,
+                lhsT=codes[:, g * P : (g + 1) * P].bitcast(FP8X4),
+                lhsT_scale=plane[:, g * P : (g + 1) * P],
+                rhs=rhs.bitcast(FP8X4),
+                rhs_scale=rhs_scale,
+                start=first,
+                stop=last,
+            )
+
+        acc = {}
+
+        def mix_tile(i):
+            if i == LAST - 1:
+                acc[i] = ps_score.tile([P, D], F32, name="sc")
+            else:
+                acc[i] = ps_out.tile([P, D], F32, name="o")
+            for n, g in enumerate((1, 2, 0)):
+                mix(i, acc[i][:], g, n == 0, n == 2)
+
+        def store(i, o, lo, hi, engine):
+            b, r = divmod(i, TPB)
+            res = results.tile([P, hi - lo], F32, name="res")
+            copy_on(engine, res[:], o)
+            nc.sync.dma_start(out=out[b, r * P : (r + 1) * P, lo:hi], in_=res[:])
+
+
+        SHARE = ()
+        turn_rows(q_raw[0], q_grp[0], 0, 1, nc.scalar)
+        quantize(q_codes[0], q_plane[0], q_grp[0], 0, P)
+        score(0, 1)
+        score(0, 2)
+        row_max(0, 1)
+        turn_rows(k_raw[0], k_grp[0], 0, 2, nc.scalar)
+        row_max(0, 2)
+        own_shift(0, 1)
+        own_shift(0, 2)
+        turn_rows(k_raw[0], k_grp[0], 2, 2, nc.vector)
+        exponentials(0, 1, nm[0][:, 1:2])
+        turn_rows(q_raw[0], q_grp[0], 1, 2, nc.scalar)
+        quantize(k_codes[0], k_plane[0], k_grp[0], 0, S)
+        exponentials(0, 2, nm[0][:, 2:3])
+        score(0, 0)
+        quantize(q_codes[0], q_plane[0], q_grp[0], P, 3 * P)
+        row_max(0, 0)
+        score(1, 1)
+        score(1, 2)
+        row_max(1, 1)
+        own_shift(0, 0)
+        exponentials(0, 0, nm[0][:, 0:1])
+        z_join(0)
+        score(1, 0)
+        turn_rows(q_raw[0], q_grp[0], 3, 1, nc.scalar)
+        widen_v(0, 0, nc.scalar)
+
+        for s in range(1, NT):
+            last = s == LAST
+            if s >= 2:
+                copy_probs(s - 2, 1, 3, nc.scalar)
+            if s > 1:
+                row_max(s, 1)
+            if last:
+                own_shift(s, 1)
+                exponentials(s, 1, nm[s][:, 1:2])
+            if s >= 2:
+                copy_probs(s - 2, 0, 1, nc.scalar)
+            row_max(s, 2)
+            if s == 1:
+                z_weigh(0)
+            z_sum(s - 1)
+            if last:
+                own_shift(s, 2)
+                exponentials(s, 2, nm[s][:, 2:3])
+            row_max(s, 0)
+            z_inv(s - 1)
+            if last:
+                own_shift(s, 0)
+            else:
+                j = join_shift(s, m3[s])
+            z_factors(s - 1)
+            if s - 1 in SHARE:
+                factor_last(s - 1, 0)
+            if s >= 3:
+                store(s - 3, acc[s - 3][:], 0, D, nc.scalar)
+            if last:
+                exponentials(s, 0, nm[s][:, 0:1])
+                z_join(s)
+            else:
+                for c in CHUNKS:
+                    exponentials(s, c, j[:])
+                if s in SHARE:
+                    gain_first(s, 0)
+            if s == 3:
+                quantize(k_codes[1], k_plane[1], k_grp[1], 0, S)
+                quantize(q_codes[1], q_plane[1], q_grp[1], 0 * P, 2 * P)
+            normalise(s - 1, 1)
+            normalise(s - 1, 2)
+            if s - 1 not in SHARE:
+                normalise(s - 1, 0)
+            if last:
+                z_weigh(s)
+            if s >= 2:
+                quantize_probs(s - 2, 1, 3)
+            if last:
+                z_sum(s)
+            if s >= 2:
+                quantize_probs(s - 2, 0, 1)
+            if s == 1:
+                widen_v(0, 1, nc.scalar)
+                widen_v(0, 2, nc.scalar)
+                widen_v(0, 3, nc.scalar)
+                interleave_v(0, 0, nc.gpsimd)
+                interleave_v(0, 1, nc.gpsimd)
+                quantize(q_codes[0], q_plane[0], q_grp[0], 3 * P, S)
+            if s == 2:
+                turn_rows(k_raw[1], k_grp[1], 0, 2, nc.scalar)
+                turn_rows(k_raw[1], k_grp[1], 2, 2, nc.scalar)
+                turn_rows(q_raw[1], q_grp[1], 0, 2, nc.scalar)
+                quantize(v_codes[0], v_plane[0], v_grp[0], 0, D)
+            if s == 3:
+                turn_rows(q_raw[1], q_grp[1], 2, 2, nc.scalar)
+            if s == 4:
+                widen_v(1, 0, nc.scalar)
+                widen_v(1, 1, nc.scalar)
+                widen_v(1, 2, nc.scalar)
+                quantize(q_codes[1], q_plane[1], q_grp[1], 2 * P, 4 * P)
+            if s == 5:
+                widen_v(1, 3, nc.scalar)
+                interleave_v(1, 0, nc.gpsimd)
+                interleave_v(1, 1, nc.gpsimd)
+            if s == 6:
+                quantize(v_codes[1], v_plane[1], v_grp[1], 0, D)
+            if not last:
+                for c in CHUNKS:
+                    score(s + 1, c)
+            turn_probs(s - 1, 1, 3)
+            turn_probs(s - 1, 0, 1)
+            if s >= 2:
+                mix_tile(s - 2)
+
+        copy_probs(LAST - 1, 1, 3, nc.scalar)
+        z_inv(LAST)
+        quantize_probs(LAST - 1, 1, 3)
+        z_factors(LAST)
+        copy_probs(LAST - 1, 0, 1, nc.scalar)
+        quantize_probs(LAST - 1, 0, 1)
+        mix_tile(LAST - 1)
+        normalise(LAST, 1)
+        normalise(LAST, 2)
+        normalise(LAST, 0)
+        turn_probs(LAST, 1, 2)
+        turn_probs(LAST, 2, 3)
+        turn_probs(LAST, 0, 1)
+        copy_probs(LAST, 1, 2, nc.scalar)
+        copy_probs(LAST, 2, 3, nc.scalar)
+        copy_probs(LAST, 0, 1, nc.vector)
+        store(LAST - 2, acc[LAST - 2][:], 0, D, nc.scalar)
+        quantize_probs(LAST, 1, 2)
+        quantize_probs(LAST, 2, 3)
+        quantize_probs(LAST, 0, 1)
+        left = ps_score.tile([P, 512], F32, name="sc")
+        right = ps_score.tile([P, 512], F32, name="sc")
+        for n, g in enumerate((1, 2, 0)):
+            mix(LAST, left[:, 0:256], g, n == 0, n == 2, 0, 256)
+            mix(LAST, right[:, 0:256], g, n == 0, n == 2, 256, 512)
+        store(LAST - 1, acc[LAST - 1][:], 0, D, nc.scalar)
+        store(LAST, left[:, 0:256], 0, 256, nc.scalar)
+        store(LAST, right[:, 0:256], 256, 512, nc.vector)

@@ -40,6 +40,8 @@ def tile_persistentmemoryallattentionsignedgains_d1p_kernel(
         ps_out = ctx.enter_context(tc.psum_pool(name="ps_out", bufs=1))
         ctx.enter_context(tc.manual_schedule())
 
+        gain_rows = const.tile([P, W], BF16, name="gain_rows")
+        nc.vector.memset(gain_rows[:].bitcast(I32), 0)
         mk_plane = const.tile([P, M], U8, align_bytes=64, name="mk_plane")
         mv_plane = const.tile([P, D], U8, align_bytes=64, name="mv_plane")
         nc.vector.memset(mk_plane[:].bitcast(I32), 0)
@@ -56,20 +58,24 @@ def tile_persistentmemoryallattentionsignedgains_d1p_kernel(
         mv_codes = const.tile([P, 2, D], I32, align_bytes=64, name="mv_codes")
         v_sc = const.tile([P, B, 16], F32, name="v_sc")
         gains = const.tile([P, W], BF16, name="gains")
+        ones = const.tile([P, P], BF16, name="ones")
+        nc.vector.memset(ones[:], 1.0)
+        nc.scalar.dma_start(out=gain_rows[0:1, 0:S], in_=t.rearrange("(o n) -> o n", o=1))
+        nc.scalar.dma_start(out=gain_rows[0:1, S:W], in_=u.rearrange("(o n) -> o n", o=1))
 
         def load_rows(dst, src, lo, hi):
             nc.sync.dma_start(out=dst[:, lo:hi, :], in_=src.rearrange("(r p) d -> p r d", p=P)[:, lo:hi, :])
 
         load_rows(q_raw[0], q[0], 0, 1)
+        for quad in range(4):
+            nc.sync.dma_start(
+                out=mk_plane[32 * quad : 32 * quad + 4, :].bitcast(I32),
+                in_=mk_scales[0, 4 * quad : 4 * quad + 4, :].bitcast(I32),
+            )
         for h in range(2):
             nc.sync.dma_start(
                 out=mk_codes[:, h * 512 : (h + 1) * 512],
                 in_=mk_words[0, :, h * 512 : (h + 1) * 512, :].rearrange("p n t -> p (n t)").bitcast(I32),
-            )
-        for quad in range(4):
-            nc.scalar.dma_start(
-                out=mk_plane[32 * quad : 32 * quad + 4, :].bitcast(I32),
-                in_=mk_scales[0, 4 * quad : 4 * quad + 4, :].bitcast(I32),
             )
         nc.scalar.activation(out=warm[:], in_=warm[:], func=ACT.Exp)
         load_rows(k_raw[0], k[0], 0, 2)
@@ -77,8 +83,6 @@ def tile_persistentmemoryallattentionsignedgains_d1p_kernel(
         load_rows(q_raw[0], q[0], 1, 4)
         nc.sync.dma_start(out=v_sc[:], in_=v_scale.rearrange("b (p t) c -> p b (t c)", t=4))
         nc.sync.dma_start(out=v_raw[0][:], in_=v_bytes[0].rearrange("(p t) n -> p (t n)", t=4))
-        nc.sync.dma_start(out=gains[:, 0:S], in_=t.partition_broadcast(P))
-        nc.sync.dma_start(out=gains[:, S:W], in_=u.partition_broadcast(P))
         load_rows(k_raw[1], k[1], 0, 4)
         for g in range(2):
             nc.sync.dma_start(out=mv_codes[:, g, :], in_=mv_words[g].rearrange("p n t -> p (n t)").bitcast(I32))
@@ -313,7 +317,6 @@ def tile_persistentmemoryallattentionsignedgains_d1p_kernel(
             nc.sync.dma_start(out=out[b, r * P : (r + 1) * P, lo:hi], in_=res[:])
 
 
-        SHARE = ()
         turn_rows(q_raw[0], q_grp[0], 0, 1, nc.scalar)
         quantize(q_codes[0], q_plane[0], q_grp[0], 0, P)
         score(0, 1)
@@ -328,8 +331,17 @@ def tile_persistentmemoryallattentionsignedgains_d1p_kernel(
         turn_rows(q_raw[0], q_grp[0], 1, 2, nc.scalar)
         quantize(k_codes[0], k_plane[0], k_grp[0], 0, S)
         exponentials(0, 2, nm[0][:, 2:3])
+        spread = [
+            ps_turn.tile([P, 512], F32, name="bank") if c > 0 else ps_out.tile([P, 512], F32, name="o") for c in range(3)
+        ]
+        for c in CHUNKS:
+            nc.tensor.matmul(
+                spread[c][:], lhsT=ones[:], rhs=gain_rows[:, c * 512 : (c + 1) * 512], start=True, stop=True
+            )
         score(0, 0)
         quantize(q_codes[0], q_plane[0], q_grp[0], P, 3 * P)
+        for c in CHUNKS:
+            nc.scalar.copy(out=gains[:, c * 512 : (c + 1) * 512], in_=spread[c][:])
         row_max(0, 0)
         score(1, 1)
         score(1, 2)
@@ -340,92 +352,178 @@ def tile_persistentmemoryallattentionsignedgains_d1p_kernel(
         score(1, 0)
         turn_rows(q_raw[0], q_grp[0], 3, 1, nc.scalar)
         widen_v(0, 0, nc.scalar)
-
-        for s in range(1, NT):
-            last = s == LAST
-            if s >= 2:
-                copy_probs(s - 2, 1, 3, nc.scalar)
-            if s > 1:
-                row_max(s, 1)
-            if last:
-                own_shift(s, 1)
-                exponentials(s, 1, nm[s][:, 1:2])
-            if s >= 2:
-                copy_probs(s - 2, 0, 1, nc.scalar)
-            row_max(s, 2)
-            if s == 1:
-                z_weigh(0)
-            z_sum(s - 1)
-            if last:
-                own_shift(s, 2)
-                exponentials(s, 2, nm[s][:, 2:3])
-            row_max(s, 0)
-            z_inv(s - 1)
-            if last:
-                own_shift(s, 0)
-            else:
-                j = join_shift(s, m3[s])
-            z_factors(s - 1)
-            if s - 1 in SHARE:
-                factor_last(s - 1, 0)
-            if s >= 3:
-                store(s - 3, acc[s - 3][:], 0, D, nc.scalar)
-            if last:
-                exponentials(s, 0, nm[s][:, 0:1])
-                z_join(s)
-            else:
-                for c in CHUNKS:
-                    exponentials(s, c, j[:])
-                if s in SHARE:
-                    gain_first(s, 0)
-            if s == 3:
-                quantize(k_codes[1], k_plane[1], k_grp[1], 0, S)
-                quantize(q_codes[1], q_plane[1], q_grp[1], 0 * P, 2 * P)
-            normalise(s - 1, 1)
-            normalise(s - 1, 2)
-            if s - 1 not in SHARE:
-                normalise(s - 1, 0)
-            if last:
-                z_weigh(s)
-            if s >= 2:
-                quantize_probs(s - 2, 1, 3)
-            if last:
-                z_sum(s)
-            if s >= 2:
-                quantize_probs(s - 2, 0, 1)
-            if s == 1:
-                widen_v(0, 1, nc.scalar)
-                widen_v(0, 2, nc.scalar)
-                widen_v(0, 3, nc.scalar)
-                interleave_v(0, 0, nc.gpsimd)
-                interleave_v(0, 1, nc.gpsimd)
-                quantize(q_codes[0], q_plane[0], q_grp[0], 3 * P, S)
-            if s == 2:
-                turn_rows(k_raw[1], k_grp[1], 0, 2, nc.scalar)
-                turn_rows(k_raw[1], k_grp[1], 2, 2, nc.scalar)
-                turn_rows(q_raw[1], q_grp[1], 0, 2, nc.scalar)
-                quantize(v_codes[0], v_plane[0], v_grp[0], 0, D)
-            if s == 3:
-                turn_rows(q_raw[1], q_grp[1], 2, 2, nc.scalar)
-            if s == 4:
-                widen_v(1, 0, nc.scalar)
-                widen_v(1, 1, nc.scalar)
-                widen_v(1, 2, nc.scalar)
-                quantize(q_codes[1], q_plane[1], q_grp[1], 2 * P, 4 * P)
-            if s == 5:
-                widen_v(1, 3, nc.scalar)
-                interleave_v(1, 0, nc.gpsimd)
-                interleave_v(1, 1, nc.gpsimd)
-            if s == 6:
-                quantize(v_codes[1], v_plane[1], v_grp[1], 0, D)
-            if not last:
-                for c in CHUNKS:
-                    score(s + 1, c)
-            turn_probs(s - 1, 1, 3)
-            turn_probs(s - 1, 0, 1)
-            if s >= 2:
-                mix_tile(s - 2)
-
+        row_max(1, 2)
+        z_weigh(0)
+        z_sum(0)
+        row_max(1, 0)
+        z_inv(0)
+        j = join_shift(1, m3[1])
+        z_factors(0)
+        turn_rows(k_raw[1], k_grp[1], 0, 2, nc.scalar)
+        quantize(q_codes[0], q_plane[0], q_grp[0], 3 * P, S)
+        for c in CHUNKS:
+            exponentials(1, c, j[:])
+        normalise(0, 1)
+        normalise(0, 2)
+        normalise(0, 0)
+        turn_rows(k_raw[1], k_grp[1], 2, 2, nc.scalar)
+        widen_v(0, 1, nc.scalar)
+        widen_v(0, 2, nc.scalar)
+        for c in CHUNKS:
+            score(2, c)
+        turn_probs(0, 1, 3)
+        turn_probs(0, 0, 1)
+        copy_probs(0, 1, 3, nc.scalar)
+        row_max(2, 1)
+        copy_probs(0, 0, 1, nc.scalar)
+        row_max(2, 2)
+        z_sum(1)
+        row_max(2, 0)
+        z_inv(1)
+        j = join_shift(2, m3[2])
+        z_factors(1)
+        turn_rows(q_raw[1], q_grp[1], 0, 2, nc.scalar)
+        widen_v(0, 3, nc.scalar)
+        for c in CHUNKS:
+            exponentials(2, c, j[:])
+        normalise(1, 1)
+        normalise(1, 2)
+        normalise(1, 0)
+        quantize_probs(0, 1, 3)
+        quantize_probs(0, 0, 1)
+        turn_rows(q_raw[1], q_grp[1], 2, 2, nc.scalar)
+        interleave_v(0, 0, nc.vector)
+        interleave_v(0, 1, nc.vector)
+        quantize(v_codes[0], v_plane[0], v_grp[0], 0, D)
+        quantize(q_codes[1], q_plane[1], q_grp[1], 0 * P, 2 * P)
+        for c in CHUNKS:
+            score(3, c)
+        turn_probs(1, 1, 3)
+        turn_probs(1, 0, 1)
+        mix_tile(0)
+        widen_v(1, 2, nc.scalar)
+        quantize(k_codes[1], k_plane[1], k_grp[1], 0, S)
+        copy_probs(1, 1, 3, nc.scalar)
+        row_max(3, 1)
+        copy_probs(1, 0, 1, nc.scalar)
+        row_max(3, 2)
+        z_sum(2)
+        row_max(3, 0)
+        z_inv(2)
+        j = join_shift(3, m3[3])
+        z_factors(2)
+        store(0, acc[0][:], 0, D, nc.scalar)
+        for c in CHUNKS:
+            exponentials(3, c, j[:])
+        normalise(2, 1)
+        normalise(2, 2)
+        normalise(2, 0)
+        quantize_probs(1, 1, 3)
+        quantize_probs(1, 0, 1)
+        for c in CHUNKS:
+            score(4, c)
+        turn_probs(2, 1, 3)
+        turn_probs(2, 0, 1)
+        mix_tile(1)
+        copy_probs(2, 1, 3, nc.scalar)
+        row_max(4, 1)
+        copy_probs(2, 0, 1, nc.scalar)
+        row_max(4, 2)
+        z_sum(3)
+        row_max(4, 0)
+        z_inv(3)
+        j = join_shift(4, m3[4])
+        z_factors(3)
+        store(1, acc[1][:], 0, D, nc.scalar)
+        for c in CHUNKS:
+            exponentials(4, c, j[:])
+        normalise(3, 1)
+        normalise(3, 2)
+        normalise(3, 0)
+        quantize_probs(2, 1, 3)
+        quantize_probs(2, 0, 1)
+        quantize(q_codes[1], q_plane[1], q_grp[1], 2 * P, 4 * P)
+        for c in CHUNKS:
+            score(5, c)
+        turn_probs(3, 1, 3)
+        turn_probs(3, 0, 1)
+        mix_tile(2)
+        widen_v(1, 0, nc.scalar)
+        copy_probs(3, 1, 3, nc.scalar)
+        row_max(5, 1)
+        copy_probs(3, 0, 1, nc.scalar)
+        row_max(5, 2)
+        z_sum(4)
+        row_max(5, 0)
+        z_inv(4)
+        j = join_shift(5, m3[5])
+        z_factors(4)
+        store(2, acc[2][:], 0, D, nc.scalar)
+        for c in CHUNKS:
+            exponentials(5, c, j[:])
+        normalise(4, 1)
+        normalise(4, 2)
+        normalise(4, 0)
+        quantize_probs(3, 1, 3)
+        quantize_probs(3, 0, 1)
+        for c in CHUNKS:
+            score(6, c)
+        turn_probs(4, 1, 3)
+        turn_probs(4, 0, 1)
+        mix_tile(3)
+        widen_v(1, 1, nc.scalar)
+        widen_v(1, 3, nc.scalar)
+        interleave_v(1, 0, nc.scalar)
+        copy_probs(4, 1, 3, nc.scalar)
+        row_max(6, 1)
+        copy_probs(4, 0, 1, nc.scalar)
+        row_max(6, 2)
+        z_sum(5)
+        row_max(6, 0)
+        z_inv(5)
+        j = join_shift(6, m3[6])
+        z_factors(5)
+        store(3, acc[3][:], 0, D, nc.scalar)
+        interleave_v(1, 1, nc.vector)
+        for c in CHUNKS:
+            exponentials(6, c, j[:])
+        normalise(5, 1)
+        normalise(5, 2)
+        normalise(5, 0)
+        quantize_probs(4, 1, 3)
+        quantize_probs(4, 0, 1)
+        quantize(v_codes[1], v_plane[1], v_grp[1], 0, D)
+        for c in CHUNKS:
+            score(7, c)
+        turn_probs(5, 1, 3)
+        turn_probs(5, 0, 1)
+        mix_tile(4)
+        copy_probs(5, 1, 3, nc.scalar)
+        row_max(7, 1)
+        own_shift(7, 1)
+        exponentials(7, 1, nm[7][:, 1:2])
+        copy_probs(5, 0, 1, nc.scalar)
+        row_max(7, 2)
+        z_sum(6)
+        own_shift(7, 2)
+        exponentials(7, 2, nm[7][:, 2:3])
+        row_max(7, 0)
+        z_inv(6)
+        own_shift(7, 0)
+        z_factors(6)
+        store(4, acc[4][:], 0, D, nc.scalar)
+        exponentials(7, 0, nm[7][:, 0:1])
+        z_join(7)
+        normalise(6, 1)
+        normalise(6, 2)
+        normalise(6, 0)
+        z_weigh(7)
+        quantize_probs(5, 1, 3)
+        z_sum(7)
+        quantize_probs(5, 0, 1)
+        turn_probs(6, 1, 3)
+        turn_probs(6, 0, 1)
+        mix_tile(5)
         copy_probs(LAST - 1, 1, 3, nc.scalar)
         z_inv(LAST)
         quantize_probs(LAST - 1, 1, 3)

@@ -67,6 +67,8 @@ def tile_persistentmemoryallattentionsignedgains_d1p_kernel(
             nc.sync.dma_start(out=dst[:, lo:hi, :], in_=src.rearrange("(r p) d -> p r d", p=P)[:, lo:hi, :])
 
         load_rows(q_raw[0], q[0], 0, 1)
+        nc.sync.dma_start(out=v_sc[:], in_=v_scale.rearrange("b (p t) c -> p b (t c)", t=4))
+        nc.sync.dma_start(out=v_raw[0][:], in_=v_bytes[0].rearrange("(p t) n -> p (t n)", t=4))
         for quad in range(4):
             nc.sync.dma_start(
                 out=mk_plane[32 * quad : 32 * quad + 4, :].bitcast(I32),
@@ -81,8 +83,6 @@ def tile_persistentmemoryallattentionsignedgains_d1p_kernel(
         load_rows(k_raw[0], k[0], 0, 2)
         load_rows(k_raw[0], k[0], 2, 4)
         load_rows(q_raw[0], q[0], 1, 4)
-        nc.sync.dma_start(out=v_sc[:], in_=v_scale.rearrange("b (p t) c -> p b (t c)", t=4))
-        nc.sync.dma_start(out=v_raw[0][:], in_=v_bytes[0].rearrange("(p t) n -> p (t n)", t=4))
         load_rows(k_raw[1], k[1], 0, 4)
         for g in range(2):
             nc.sync.dma_start(out=mv_codes[:, g, :], in_=mv_words[g].rearrange("p n t -> p (n t)").bitcast(I32))
@@ -147,8 +147,9 @@ def tile_persistentmemoryallattentionsignedgains_d1p_kernel(
                     )
 
         def interleave_v(b, h, engine):
-            cols = slice(h * D // 2, (h + 1) * D // 2)
-            dst, src = v_grp[b][:, cols, :], v_wide[b][:, :, cols].rearrange("p f n -> p n f")
+            cols = slice(h * 256, (h + 1) * 256)
+            dst = v_grp[b][:, cols, :].rearrange("p (c i) f -> p c f i", i=4)
+            src = v_wide[b][:, :, cols].rearrange("p f (c i) -> p c f i", i=4)
             if engine is nc.gpsimd:
                 nc.gpsimd.tensor_scalar(out=dst, in0=src, scalar1=1.0, scalar2=0.0, op0=ALU.mult, op1=ALU.add)
             else:
@@ -252,11 +253,11 @@ def tile_persistentmemoryallattentionsignedgains_d1p_kernel(
                 out=probs[i][:, c * 512 : (c + 1) * 512], in_=gained[i][:], func=ACT.Copy, scale=fac[i][c]
             )
 
-        def normalise(i, c):
+        def normalise(i, lo, hi):
             probs_tile(i)
-            cols = slice(c * 512, (c + 1) * 512)
+            cols = slice(lo * 512, hi * 512)
             nc.vector.scalar_tensor_tensor(
-                out=probs[i][:, cols], in0=ex[i][:, cols], scalar=fac[i][c], in1=gains[:, cols], op0=ALU.mult, op1=ALU.mult
+                out=probs[i][:, cols], in0=ex[i][:, cols], scalar=fac[i][lo], in1=gains[:, cols], op0=ALU.mult, op1=ALU.mult
             )
 
         def turn_probs(i, lo, hi):
@@ -319,8 +320,12 @@ def tile_persistentmemoryallattentionsignedgains_d1p_kernel(
 
         turn_rows(q_raw[0], q_grp[0], 0, 1, nc.scalar)
         quantize(q_codes[0], q_plane[0], q_grp[0], 0, P)
+        widen_v(0, 0, nc.scalar)
+        widen_v(0, 1, nc.vector)
+        widen_v(0, 3, nc.vector)
         score(0, 1)
         score(0, 2)
+        widen_v(0, 2, nc.scalar)
         row_max(0, 1)
         turn_rows(k_raw[0], k_grp[0], 0, 2, nc.scalar)
         row_max(0, 2)
@@ -331,95 +336,90 @@ def tile_persistentmemoryallattentionsignedgains_d1p_kernel(
         turn_rows(q_raw[0], q_grp[0], 1, 2, nc.scalar)
         quantize(k_codes[0], k_plane[0], k_grp[0], 0, S)
         exponentials(0, 2, nm[0][:, 2:3])
-        spread = [
-            ps_turn.tile([P, 512], F32, name="bank") if c > 0 else ps_out.tile([P, 512], F32, name="o") for c in range(3)
-        ]
-        for c in CHUNKS:
-            nc.tensor.matmul(
-                spread[c][:], lhsT=ones[:], rhs=gain_rows[:, c * 512 : (c + 1) * 512], start=True, stop=True
-            )
         score(0, 0)
         quantize(q_codes[0], q_plane[0], q_grp[0], P, 3 * P)
-        for c in CHUNKS:
-            nc.scalar.copy(out=gains[:, c * 512 : (c + 1) * 512], in_=spread[c][:])
+        interleave_v(0, 0, nc.scalar)
         row_max(0, 0)
         score(1, 1)
         score(1, 2)
-        row_max(1, 1)
         own_shift(0, 0)
+        row_max(1, 1)
         exponentials(0, 0, nm[0][:, 0:1])
         z_join(0)
         score(1, 0)
         turn_rows(q_raw[0], q_grp[0], 3, 1, nc.scalar)
-        widen_v(0, 0, nc.scalar)
-        row_max(1, 2)
+        spread_m = ps_turn.tile([P, M], BF16, name="bank")
+        spread_c = ps_out.tile([P, S], BF16, name="o")
+        for lo, bank in ((0, spread_c[:]), (S, spread_m[:, 0:512]), (S + 512, spread_m[:, 512:1024])):
+            nc.tensor.matmul(bank, lhsT=ones[:], rhs=gain_rows[:, lo : lo + 512], start=True, stop=True)
+        nc.scalar.copy(out=gains[:, S:W], in_=spread_m[:])
+        nc.scalar.copy(out=gains[:, 0:S], in_=spread_c[:])
+        turn_rows(q_raw[1], q_grp[1], 0, 2, nc.scalar)
+        interleave_v(0, 1, nc.vector)
         z_weigh(0)
+        row_max(1, 2)
         z_sum(0)
         row_max(1, 0)
         z_inv(0)
+        turn_rows(k_raw[1], k_grp[1], 2, 2, nc.scalar)
+        quantize(q_codes[0], q_plane[0], q_grp[0], 3 * P, S)
         j = join_shift(1, m3[1])
         z_factors(0)
-        turn_rows(k_raw[1], k_grp[1], 0, 2, nc.scalar)
-        quantize(q_codes[0], q_plane[0], q_grp[0], 3 * P, S)
         for c in CHUNKS:
             exponentials(1, c, j[:])
-        normalise(0, 1)
-        normalise(0, 2)
-        normalise(0, 0)
-        turn_rows(k_raw[1], k_grp[1], 2, 2, nc.scalar)
-        widen_v(0, 1, nc.scalar)
-        widen_v(0, 2, nc.scalar)
+        normalise(0, 1, 2)
+        normalise(0, 2, 3)
+        normalise(0, 0, 1)
         for c in CHUNKS:
             score(2, c)
         turn_probs(0, 1, 3)
         turn_probs(0, 0, 1)
+        turn_rows(k_raw[1], k_grp[1], 0, 2, nc.scalar)
+        turn_rows(q_raw[1], q_grp[1], 2, 2, nc.scalar)
+        quantize(v_codes[0], v_plane[0], v_grp[0], 0, D)
         copy_probs(0, 1, 3, nc.scalar)
         row_max(2, 1)
         copy_probs(0, 0, 1, nc.scalar)
-        row_max(2, 2)
         z_sum(1)
-        row_max(2, 0)
+        row_max(2, 2)
         z_inv(1)
-        j = join_shift(2, m3[2])
+        row_max(2, 0)
         z_factors(1)
-        turn_rows(q_raw[1], q_grp[1], 0, 2, nc.scalar)
-        widen_v(0, 3, nc.scalar)
+        quantize(k_codes[1], k_plane[1], k_grp[1], 0, S)
+        j = join_shift(2, m3[2])
         for c in CHUNKS:
             exponentials(2, c, j[:])
-        normalise(1, 1)
-        normalise(1, 2)
-        normalise(1, 0)
+        normalise(1, 1, 2)
+        normalise(1, 2, 3)
+        normalise(1, 0, 1)
         quantize_probs(0, 1, 3)
         quantize_probs(0, 0, 1)
-        turn_rows(q_raw[1], q_grp[1], 2, 2, nc.scalar)
-        interleave_v(0, 0, nc.vector)
-        interleave_v(0, 1, nc.vector)
-        quantize(v_codes[0], v_plane[0], v_grp[0], 0, D)
-        quantize(q_codes[1], q_plane[1], q_grp[1], 0 * P, 2 * P)
         for c in CHUNKS:
             score(3, c)
         turn_probs(1, 1, 3)
         turn_probs(1, 0, 1)
         mix_tile(0)
-        widen_v(1, 2, nc.scalar)
-        quantize(k_codes[1], k_plane[1], k_grp[1], 0, S)
+        widen_v(1, 1, nc.scalar)
         copy_probs(1, 1, 3, nc.scalar)
         row_max(3, 1)
         copy_probs(1, 0, 1, nc.scalar)
-        row_max(3, 2)
         z_sum(2)
-        row_max(3, 0)
+        row_max(3, 2)
         z_inv(2)
-        j = join_shift(3, m3[3])
+        row_max(3, 0)
         z_factors(2)
         store(0, acc[0][:], 0, D, nc.scalar)
+        quantize(q_codes[1], q_plane[1], q_grp[1], 0 * P, 2 * P)
+        j = join_shift(3, m3[3])
         for c in CHUNKS:
             exponentials(3, c, j[:])
-        normalise(2, 1)
-        normalise(2, 2)
-        normalise(2, 0)
+        normalise(2, 1, 2)
+        normalise(2, 2, 3)
+        normalise(2, 0, 1)
         quantize_probs(1, 1, 3)
         quantize_probs(1, 0, 1)
+        widen_v(1, 0, nc.scalar)
+        widen_v(1, 2, nc.scalar)
         for c in CHUNKS:
             score(4, c)
         turn_probs(2, 1, 3)
@@ -428,68 +428,66 @@ def tile_persistentmemoryallattentionsignedgains_d1p_kernel(
         copy_probs(2, 1, 3, nc.scalar)
         row_max(4, 1)
         copy_probs(2, 0, 1, nc.scalar)
-        row_max(4, 2)
         z_sum(3)
-        row_max(4, 0)
+        row_max(4, 2)
         z_inv(3)
-        j = join_shift(4, m3[4])
+        row_max(4, 0)
         z_factors(3)
         store(1, acc[1][:], 0, D, nc.scalar)
+        j = join_shift(4, m3[4])
         for c in CHUNKS:
             exponentials(4, c, j[:])
-        normalise(3, 1)
-        normalise(3, 2)
-        normalise(3, 0)
+        normalise(3, 1, 2)
+        normalise(3, 2, 3)
+        normalise(3, 0, 1)
         quantize_probs(2, 1, 3)
         quantize_probs(2, 0, 1)
-        quantize(q_codes[1], q_plane[1], q_grp[1], 2 * P, 4 * P)
         for c in CHUNKS:
             score(5, c)
         turn_probs(3, 1, 3)
         turn_probs(3, 0, 1)
         mix_tile(2)
-        widen_v(1, 0, nc.scalar)
         copy_probs(3, 1, 3, nc.scalar)
         row_max(5, 1)
         copy_probs(3, 0, 1, nc.scalar)
-        row_max(5, 2)
         z_sum(4)
-        row_max(5, 0)
+        row_max(5, 2)
         z_inv(4)
-        j = join_shift(5, m3[5])
+        row_max(5, 0)
         z_factors(4)
         store(2, acc[2][:], 0, D, nc.scalar)
+        quantize(q_codes[1], q_plane[1], q_grp[1], 2 * P, 4 * P)
+        j = join_shift(5, m3[5])
         for c in CHUNKS:
             exponentials(5, c, j[:])
-        normalise(4, 1)
-        normalise(4, 2)
-        normalise(4, 0)
+        normalise(4, 1, 2)
+        normalise(4, 2, 3)
+        normalise(4, 0, 1)
         quantize_probs(3, 1, 3)
         quantize_probs(3, 0, 1)
+        widen_v(1, 3, nc.scalar)
+        interleave_v(1, 0, nc.scalar)
         for c in CHUNKS:
             score(6, c)
         turn_probs(4, 1, 3)
         turn_probs(4, 0, 1)
         mix_tile(3)
-        widen_v(1, 1, nc.scalar)
-        widen_v(1, 3, nc.scalar)
-        interleave_v(1, 0, nc.scalar)
         copy_probs(4, 1, 3, nc.scalar)
         row_max(6, 1)
         copy_probs(4, 0, 1, nc.scalar)
-        row_max(6, 2)
         z_sum(5)
-        row_max(6, 0)
+        row_max(6, 2)
         z_inv(5)
-        j = join_shift(6, m3[6])
+        row_max(6, 0)
         z_factors(5)
         store(3, acc[3][:], 0, D, nc.scalar)
         interleave_v(1, 1, nc.vector)
+        j = join_shift(6, m3[6])
         for c in CHUNKS:
             exponentials(6, c, j[:])
-        normalise(5, 1)
-        normalise(5, 2)
-        normalise(5, 0)
+        normalise(5, 1, 2)
+        normalise(5, 2, 3)
+        normalise(5, 0, 1)
         quantize_probs(4, 1, 3)
         quantize_probs(4, 0, 1)
         quantize(v_codes[1], v_plane[1], v_grp[1], 0, D)
@@ -500,23 +498,23 @@ def tile_persistentmemoryallattentionsignedgains_d1p_kernel(
         mix_tile(4)
         copy_probs(5, 1, 3, nc.scalar)
         row_max(7, 1)
+        copy_probs(5, 0, 1, nc.scalar)
+        z_sum(6)
         own_shift(7, 1)
         exponentials(7, 1, nm[7][:, 1:2])
-        copy_probs(5, 0, 1, nc.scalar)
         row_max(7, 2)
-        z_sum(6)
+        z_inv(6)
         own_shift(7, 2)
         exponentials(7, 2, nm[7][:, 2:3])
         row_max(7, 0)
-        z_inv(6)
-        own_shift(7, 0)
         z_factors(6)
         store(4, acc[4][:], 0, D, nc.scalar)
+        own_shift(7, 0)
         exponentials(7, 0, nm[7][:, 0:1])
         z_join(7)
-        normalise(6, 1)
-        normalise(6, 2)
-        normalise(6, 0)
+        normalise(6, 1, 2)
+        normalise(6, 2, 3)
+        normalise(6, 0, 1)
         z_weigh(7)
         quantize_probs(5, 1, 3)
         z_sum(7)
@@ -531,18 +529,18 @@ def tile_persistentmemoryallattentionsignedgains_d1p_kernel(
         copy_probs(LAST - 1, 0, 1, nc.scalar)
         quantize_probs(LAST - 1, 0, 1)
         mix_tile(LAST - 1)
-        normalise(LAST, 1)
-        normalise(LAST, 2)
-        normalise(LAST, 0)
+        normalise(LAST, 1, 2)
+        normalise(LAST, 2, 3)
+        normalise(LAST, 0, 1)
         turn_probs(LAST, 1, 2)
         turn_probs(LAST, 2, 3)
         turn_probs(LAST, 0, 1)
+        store(LAST - 2, acc[LAST - 2][:], 0, D, nc.scalar)
         copy_probs(LAST, 1, 2, nc.scalar)
         copy_probs(LAST, 2, 3, nc.scalar)
-        copy_probs(LAST, 0, 1, nc.vector)
-        store(LAST - 2, acc[LAST - 2][:], 0, D, nc.scalar)
         quantize_probs(LAST, 1, 2)
         quantize_probs(LAST, 2, 3)
+        copy_probs(LAST, 0, 1, nc.vector)
         quantize_probs(LAST, 0, 1)
         left = ps_score.tile([P, 512], F32, name="sc")
         right = ps_score.tile([P, 512], F32, name="sc")

@@ -222,7 +222,11 @@ def tile_persistentmemoryallattentionsignedgains_d1p_kernel(
 
         def z_sum(i):
             zs[i] = small.tile([P, 1], F32, name="zs_t")
-            nc.vector.tensor_reduce(out=zs[i][:], in_=z3[i][:], axis=AX.X, op=ALU.add)
+            if i in SPLIT:
+                nc.vector.tensor_reduce(out=zs[i][:], in_=z3[i][:], axis=AX.X, op=ALU.add)
+            else:
+                z_parts = small.tile([P, 3], F32, name="z_parts")
+                nc.scalar.activation(out=z_parts[:], in_=z3[i][:], func=ACT.Copy, accum_out=zs[i][:])
 
         def z_inv(i):
             inv = small.tile([P, 1], F32, name="inv")
@@ -320,12 +324,13 @@ def tile_persistentmemoryallattentionsignedgains_d1p_kernel(
 
         turn_rows(q_raw[0], q_grp[0], 0, 1, nc.scalar)
         quantize(q_codes[0], q_plane[0], q_grp[0], 0, P)
-        widen_v(0, 0, nc.scalar)
+        widen_v(0, 0, nc.vector)
         widen_v(0, 1, nc.vector)
-        widen_v(0, 3, nc.vector)
+        widen_v(0, 2, nc.scalar)
         score(0, 1)
         score(0, 2)
-        widen_v(0, 2, nc.scalar)
+        widen_v(0, 3, nc.vector)
+        interleave_v(0, 0, nc.vector)
         row_max(0, 1)
         turn_rows(k_raw[0], k_grp[0], 0, 2, nc.scalar)
         row_max(0, 2)
@@ -338,7 +343,7 @@ def tile_persistentmemoryallattentionsignedgains_d1p_kernel(
         exponentials(0, 2, nm[0][:, 2:3])
         score(0, 0)
         quantize(q_codes[0], q_plane[0], q_grp[0], P, 3 * P)
-        interleave_v(0, 0, nc.scalar)
+        turn_rows(k_raw[1], k_grp[1], 2, 2, nc.scalar)
         row_max(0, 0)
         score(1, 1)
         score(1, 2)
@@ -354,33 +359,32 @@ def tile_persistentmemoryallattentionsignedgains_d1p_kernel(
             nc.tensor.matmul(bank, lhsT=ones[:], rhs=gain_rows[:, lo : lo + 512], start=True, stop=True)
         nc.scalar.copy(out=gains[:, S:W], in_=spread_m[:])
         nc.scalar.copy(out=gains[:, 0:S], in_=spread_c[:])
-        turn_rows(q_raw[1], q_grp[1], 0, 2, nc.scalar)
         interleave_v(0, 1, nc.vector)
+        turn_rows(k_raw[1], k_grp[1], 0, 2, nc.scalar)
         z_weigh(0)
         row_max(1, 2)
         z_sum(0)
         row_max(1, 0)
         z_inv(0)
-        turn_rows(k_raw[1], k_grp[1], 2, 2, nc.scalar)
-        quantize(q_codes[0], q_plane[0], q_grp[0], 3 * P, S)
+        quantize(v_codes[0], v_plane[0], v_grp[0], 0, D)
         j = join_shift(1, m3[1])
         z_factors(0)
         for c in CHUNKS:
             exponentials(1, c, j[:])
+        z_sum(1)
         normalise(0, 1, 2)
         normalise(0, 2, 3)
         normalise(0, 0, 1)
+        turn_rows(q_raw[1], q_grp[1], 0, 2, nc.scalar)
+        turn_rows(q_raw[1], q_grp[1], 2, 2, nc.scalar)
+        quantize(q_codes[0], q_plane[0], q_grp[0], 3 * P, S)
         for c in CHUNKS:
             score(2, c)
         turn_probs(0, 1, 3)
         turn_probs(0, 0, 1)
-        turn_rows(k_raw[1], k_grp[1], 0, 2, nc.scalar)
-        turn_rows(q_raw[1], q_grp[1], 2, 2, nc.scalar)
-        quantize(v_codes[0], v_plane[0], v_grp[0], 0, D)
         copy_probs(0, 1, 3, nc.scalar)
         row_max(2, 1)
         copy_probs(0, 0, 1, nc.scalar)
-        z_sum(1)
         row_max(2, 2)
         z_inv(1)
         row_max(2, 0)
@@ -389,21 +393,21 @@ def tile_persistentmemoryallattentionsignedgains_d1p_kernel(
         j = join_shift(2, m3[2])
         for c in CHUNKS:
             exponentials(2, c, j[:])
+        z_sum(2)
         normalise(1, 1, 2)
         normalise(1, 2, 3)
         normalise(1, 0, 1)
         quantize_probs(0, 1, 3)
         quantize_probs(0, 0, 1)
+        widen_v(1, 0, nc.scalar)
         for c in CHUNKS:
             score(3, c)
         turn_probs(1, 1, 3)
         turn_probs(1, 0, 1)
         mix_tile(0)
-        widen_v(1, 1, nc.scalar)
         copy_probs(1, 1, 3, nc.scalar)
         row_max(3, 1)
         copy_probs(1, 0, 1, nc.scalar)
-        z_sum(2)
         row_max(3, 2)
         z_inv(2)
         row_max(3, 0)
@@ -413,30 +417,31 @@ def tile_persistentmemoryallattentionsignedgains_d1p_kernel(
         j = join_shift(3, m3[3])
         for c in CHUNKS:
             exponentials(3, c, j[:])
+        z_sum(3)
         normalise(2, 1, 2)
         normalise(2, 2, 3)
         normalise(2, 0, 1)
         quantize_probs(1, 1, 3)
         quantize_probs(1, 0, 1)
-        widen_v(1, 0, nc.scalar)
-        widen_v(1, 2, nc.scalar)
         for c in CHUNKS:
             score(4, c)
         turn_probs(2, 1, 3)
         turn_probs(2, 0, 1)
         mix_tile(1)
+        widen_v(1, 2, nc.scalar)
         copy_probs(2, 1, 3, nc.scalar)
         row_max(4, 1)
         copy_probs(2, 0, 1, nc.scalar)
-        z_sum(3)
         row_max(4, 2)
         z_inv(3)
         row_max(4, 0)
         z_factors(3)
         store(1, acc[1][:], 0, D, nc.scalar)
+        widen_v(1, 1, nc.vector)
         j = join_shift(4, m3[4])
         for c in CHUNKS:
             exponentials(4, c, j[:])
+        z_sum(4)
         normalise(3, 1, 2)
         normalise(3, 2, 3)
         normalise(3, 0, 1)
@@ -447,25 +452,25 @@ def tile_persistentmemoryallattentionsignedgains_d1p_kernel(
         turn_probs(3, 1, 3)
         turn_probs(3, 0, 1)
         mix_tile(2)
+        widen_v(1, 3, nc.scalar)
+        quantize(q_codes[1], q_plane[1], q_grp[1], 2 * P, 4 * P)
         copy_probs(3, 1, 3, nc.scalar)
         row_max(5, 1)
         copy_probs(3, 0, 1, nc.scalar)
-        z_sum(4)
         row_max(5, 2)
         z_inv(4)
         row_max(5, 0)
         z_factors(4)
         store(2, acc[2][:], 0, D, nc.scalar)
-        quantize(q_codes[1], q_plane[1], q_grp[1], 2 * P, 4 * P)
         j = join_shift(5, m3[5])
         for c in CHUNKS:
             exponentials(5, c, j[:])
+        z_sum(5)
         normalise(4, 1, 2)
         normalise(4, 2, 3)
         normalise(4, 0, 1)
         quantize_probs(3, 1, 3)
         quantize_probs(3, 0, 1)
-        widen_v(1, 3, nc.scalar)
         interleave_v(1, 0, nc.scalar)
         for c in CHUNKS:
             score(6, c)
@@ -475,7 +480,6 @@ def tile_persistentmemoryallattentionsignedgains_d1p_kernel(
         copy_probs(4, 1, 3, nc.scalar)
         row_max(6, 1)
         copy_probs(4, 0, 1, nc.scalar)
-        z_sum(5)
         row_max(6, 2)
         z_inv(5)
         row_max(6, 0)
@@ -485,6 +489,7 @@ def tile_persistentmemoryallattentionsignedgains_d1p_kernel(
         j = join_shift(6, m3[6])
         for c in CHUNKS:
             exponentials(6, c, j[:])
+        z_sum(6)
         normalise(5, 1, 2)
         normalise(5, 2, 3)
         normalise(5, 0, 1)
@@ -499,7 +504,6 @@ def tile_persistentmemoryallattentionsignedgains_d1p_kernel(
         copy_probs(5, 1, 3, nc.scalar)
         row_max(7, 1)
         copy_probs(5, 0, 1, nc.scalar)
-        z_sum(6)
         own_shift(7, 1)
         exponentials(7, 1, nm[7][:, 1:2])
         row_max(7, 2)
@@ -508,10 +512,10 @@ def tile_persistentmemoryallattentionsignedgains_d1p_kernel(
         exponentials(7, 2, nm[7][:, 2:3])
         row_max(7, 0)
         z_factors(6)
-        store(4, acc[4][:], 0, D, nc.scalar)
         own_shift(7, 0)
         exponentials(7, 0, nm[7][:, 0:1])
         z_join(7)
+        store(4, acc[4][:], 0, D, nc.scalar)
         normalise(6, 1, 2)
         normalise(6, 2, 3)
         normalise(6, 0, 1)
@@ -524,23 +528,23 @@ def tile_persistentmemoryallattentionsignedgains_d1p_kernel(
         mix_tile(5)
         copy_probs(LAST - 1, 1, 3, nc.scalar)
         z_inv(LAST)
-        quantize_probs(LAST - 1, 1, 3)
         z_factors(LAST)
         copy_probs(LAST - 1, 0, 1, nc.scalar)
-        quantize_probs(LAST - 1, 0, 1)
-        mix_tile(LAST - 1)
         normalise(LAST, 1, 2)
         normalise(LAST, 2, 3)
         normalise(LAST, 0, 1)
+        quantize_probs(LAST - 1, 1, 3)
+        quantize_probs(LAST - 1, 0, 1)
         turn_probs(LAST, 1, 2)
         turn_probs(LAST, 2, 3)
         turn_probs(LAST, 0, 1)
-        store(LAST - 2, acc[LAST - 2][:], 0, D, nc.scalar)
+        mix_tile(LAST - 1)
         copy_probs(LAST, 1, 2, nc.scalar)
         copy_probs(LAST, 2, 3, nc.scalar)
         quantize_probs(LAST, 1, 2)
         quantize_probs(LAST, 2, 3)
         copy_probs(LAST, 0, 1, nc.vector)
+        store(LAST - 2, acc[LAST - 2][:], 0, D, nc.scalar)
         quantize_probs(LAST, 0, 1)
         left = ps_score.tile([P, 512], F32, name="sc")
         right = ps_score.tile([P, 512], F32, name="sc")

@@ -19,11 +19,16 @@ ACT = mybir.ActivationFunctionType
 AX = mybir.AxisListType
 
 P = 128
+PACK = 4
+PART = 512
 W = S + M
-NT = B * S // P
-TPB = S // P
-CHUNKS = (1, 2, 0)
+ORDER = (1, 2, 0)
+ROW_TILES = S // P
+NT = B * ROW_TILES
+LAST = NT - 1
+VBLOCK = 128
 SCALE = 1.0 / math.sqrt(D)
+OWN_SHIFTS = (0, LAST)
 
 
 def tile_persistentmemoryallattentionsignedgains_d1p_kernel(
@@ -42,69 +47,70 @@ def tile_persistentmemoryallattentionsignedgains_d1p_kernel(
 
         gain_rows = const.tile([P, W], BF16, name="gain_rows")
         nc.vector.memset(gain_rows[:].bitcast(I32), 0)
-        mk_plane = const.tile([P, M], U8, align_bytes=64, name="mk_plane")
-        mv_plane = const.tile([P, D], U8, align_bytes=64, name="mv_plane")
-        nc.vector.memset(mk_plane[:].bitcast(I32), 0)
-        nc.vector.memset(mv_plane[:].bitcast(I32), 0)
-        warm = const.tile([P, 1], F32, name="warm")
-        nc.vector.memset(warm[:], 0.0)
+        mk_sc = const.tile([P, M], U8, align_bytes=64, name="mk_sc")
+        mv_sc = const.tile([P, D], U8, align_bytes=64, name="mv_sc")
+        nc.vector.memset(mk_sc[:].bitcast(I32), 0)
+        nc.vector.memset(mv_sc[:].bitcast(I32), 0)
+        zeros = const.tile([P, P], BF16, name="zeros")
+        nc.vector.memset(zeros[:], 0.0)
         ident = const.tile([P, P], F32, name="ident")
         make_identity(nc, ident[:])
 
-        q_raw = [const.tile([P, TPB, D], BF16, name="q_raw%d" % b) for b in range(B)]
-        k_raw = [const.tile([P, TPB, D], BF16, name="k_raw%d" % b) for b in range(B)]
-        v_raw = [const.tile([P, 4 * D], U8, name="v_raw%d" % b) for b in range(B)]
+        q_raw = [const.tile([P, ROW_TILES, D], BF16, name="q_raw%d" % b) for b in range(B)]
+        k_raw = [const.tile([P, ROW_TILES, D], BF16, name="k_raw%d" % b) for b in range(B)]
+        v_raw = [const.tile([P, PACK * D], U8, name="v_raw%d" % b) for b in range(B)]
         mk_codes = const.tile([P, M], I32, align_bytes=64, name="mk_codes")
         mv_codes = const.tile([P, 2, D], I32, align_bytes=64, name="mv_codes")
-        v_sc = const.tile([P, B, 16], F32, name="v_sc")
+        v_mult = const.tile([P, B, PACK * (D // VBLOCK)], F32, name="v_mult")
         gains = const.tile([P, W], BF16, name="gains")
         ones = const.tile([P, P], BF16, name="ones")
-        nc.vector.memset(ones[:], 1.0)
         nc.scalar.dma_start(out=gain_rows[0:1, 0:S], in_=t.rearrange("(o n) -> o n", o=1))
         nc.scalar.dma_start(out=gain_rows[0:1, S:W], in_=u.rearrange("(o n) -> o n", o=1))
+        nc.scalar.activation(out=ones[:], in_=zeros[:], func=ACT.Exp)
 
         def load_rows(dst, src, lo, hi):
             nc.sync.dma_start(out=dst[:, lo:hi, :], in_=src.rearrange("(r p) d -> p r d", p=P)[:, lo:hi, :])
 
+        def load_v(b):
+            nc.sync.dma_start(out=v_raw[b][:], in_=v_bytes[b].rearrange("(p t) n -> p (t n)", t=PACK))
+
+        def load_scale_rows(dst, first, rows):
+            for quarter in range(4):
+                nc.sync.dma_start(
+                    out=dst[32 * quarter + first : 32 * quarter + first + 4, :].bitcast(I32),
+                    in_=rows[4 * quarter : 4 * quarter + 4, :].bitcast(I32),
+                )
+
         load_rows(q_raw[0], q[0], 0, 1)
-        nc.sync.dma_start(out=v_sc[:], in_=v_scale.rearrange("b (p t) c -> p b (t c)", t=4))
-        nc.sync.dma_start(out=v_raw[0][:], in_=v_bytes[0].rearrange("(p t) n -> p (t n)", t=4))
-        for quad in range(4):
-            nc.sync.dma_start(
-                out=mk_plane[32 * quad : 32 * quad + 4, :].bitcast(I32),
-                in_=mk_scales[0, 4 * quad : 4 * quad + 4, :].bitcast(I32),
-            )
+        nc.sync.dma_start(out=v_mult[:], in_=v_scale.rearrange("b (p t) c -> p b (t c)", t=PACK))
+        load_v(0)
+        load_scale_rows(mk_sc, 0, mk_scales[0])
         for h in range(2):
+            cols = slice(h * PART, (h + 1) * PART)
             nc.sync.dma_start(
-                out=mk_codes[:, h * 512 : (h + 1) * 512],
-                in_=mk_words[0, :, h * 512 : (h + 1) * 512, :].rearrange("p n t -> p (n t)").bitcast(I32),
+                out=mk_codes[:, cols], in_=mk_words[0, :, cols, :].rearrange("p n t -> p (n t)").bitcast(I32)
             )
-        nc.scalar.activation(out=warm[:], in_=warm[:], func=ACT.Exp)
         load_rows(k_raw[0], k[0], 0, 2)
         load_rows(k_raw[0], k[0], 2, 4)
         load_rows(q_raw[0], q[0], 1, 4)
+        load_v(1)
         load_rows(k_raw[1], k[1], 0, 4)
         for g in range(2):
             nc.sync.dma_start(out=mv_codes[:, g, :], in_=mv_words[g].rearrange("p n t -> p (n t)").bitcast(I32))
         for g in range(2):
-            for quad in range(4):
-                nc.sync.dma_start(
-                    out=mv_plane[32 * quad + 4 * g : 32 * quad + 4 * g + 4, :].bitcast(I32),
-                    in_=mv_scales[g, 4 * quad : 4 * quad + 4, :].bitcast(I32),
-                )
+            load_scale_rows(mv_sc, 4 * g, mv_scales[g])
         load_rows(q_raw[1], q[1], 0, 4)
-        nc.sync.dma_start(out=v_raw[1][:], in_=v_bytes[1].rearrange("(p t) n -> p (t n)", t=4))
 
         q_codes = [const.tile([P, S], U32, align_bytes=64, name="q_codes%d" % b) for b in range(B)]
-        q_plane = [const.tile([P, S], U8, align_bytes=64, name="q_plane%d" % b) for b in range(B)]
+        q_sc = [const.tile([P, S], U8, align_bytes=64, name="q_sc%d" % b) for b in range(B)]
         k_codes = [const.tile([P, S], U32, align_bytes=64, name="k_codes%d" % b) for b in range(B)]
-        k_plane = [const.tile([P, S], U8, align_bytes=64, name="k_plane%d" % b) for b in range(B)]
+        k_sc = [const.tile([P, S], U8, align_bytes=64, name="k_sc%d" % b) for b in range(B)]
         v_codes = [const.tile([P, D], U32, align_bytes=64, name="v_codes%d" % b) for b in range(B)]
-        v_plane = [const.tile([P, D], U8, align_bytes=64, name="v_plane%d" % b) for b in range(B)]
-        q_grp = [const.tile([P, S, 4], BF16, align_bytes=64, name="q_grp%d" % b) for b in range(B)]
-        k_grp = [const.tile([P, S, 4], BF16, align_bytes=64, name="k_grp%d" % b) for b in range(B)]
-        v_wide = [const.tile([P, 4, D], BF16, align_bytes=64, name="v_wide%d" % b) for b in range(B)]
-        v_grp = [const.tile([P, D, 4], BF16, align_bytes=64, name="v_grp%d" % b) for b in range(B)]
+        v_sc = [const.tile([P, D], U8, align_bytes=64, name="v_sc%d" % b) for b in range(B)]
+        q_grouped = [const.tile([P, S, PACK], BF16, align_bytes=64, name="q_grouped%d" % b) for b in range(B)]
+        k_grouped = [const.tile([P, S, PACK], BF16, align_bytes=64, name="k_grouped%d" % b) for b in range(B)]
+        v_wide = [const.tile([P, PACK, D], BF16, align_bytes=64, name="v_wide%d" % b) for b in range(B)]
+        v_grouped = [const.tile([P, D, PACK], BF16, align_bytes=64, name="v_grouped%d" % b) for b in range(B)]
 
         def copy_on(engine, dst, src):
             if engine is nc.scalar:
@@ -112,445 +118,376 @@ def tile_persistentmemoryallattentionsignedgains_d1p_kernel(
             else:
                 nc.vector.tensor_copy(out=dst, in_=src)
 
-        def turn_rows(raw, grp, r0, n, engine):
-            bank = ps_turn.tile([P, n, 2, P], F32, name="bank")
-            words = raw[:].rearrange("p r d -> p (r d)").bitcast(F32)
-            half = D // 2
-            for a in range(n):
+        def quantize(codes, scales, grouped, lo, hi):
+            nc.vector.quantize_mx(
+                out=codes[:, lo:hi].bitcast(FP8X4),
+                scales=scales[:, lo:hi],
+                in_=grouped[:, lo:hi, :].rearrange("p n t -> p (n t)"),
+            )
+
+        def turn(bank, words, first, count):
+            run = PART // 2
+            for a in range(count):
                 for e in range(2):
-                    lo = (r0 + a) * half + e
-                    nc.tensor.transpose(bank[:, a, e, :], words[:, lo : (r0 + a + 1) * half : 2], ident[:])
-            dst = grp[:, r0 * P : (r0 + n) * P, :].rearrange("p n f -> p (n f)").bitcast(F32)
+                    lo = (first + a) * run
+                    nc.tensor.transpose(bank[:, a, e, :], words[:, lo + e : lo + run : 2], ident[:])
+
+        def group(engine, dst, bank):
+            count = bank.shape[1]
+            words = dst.rearrange("p n t -> p (n t)").bitcast(F32)
             copy_on(
                 engine,
-                dst.rearrange("p (a n e) -> p a n e", a=n, e=2),
+                words.rearrange("p (a n e) -> p a n e", a=count, e=2),
                 bank[:].rearrange("p a e n -> p a n e"),
             )
 
-        def quantize(codes, plane, grp, lo, hi):
-            nc.vector.quantize_mx(
-                out=codes[:, lo:hi].bitcast(FP8X4),
-                scales=plane[:, lo:hi],
-                in_=grp[:, lo:hi, :].rearrange("p n f -> p (n f)"),
+        def turn_rows(raw, grouped, r0, count, engine):
+            bank = ps_turn.tile([P, count, 2, P], F32, name="bank")
+            turn(bank, raw[:].rearrange("p r d -> p (r d)").bitcast(F32), r0, count)
+            group(engine, grouped[:, r0 * P : (r0 + count) * P, :], bank)
+
+        def quantize_q(b, r0, r1):
+            quantize(q_codes[b], q_sc[b], q_grouped[b], r0 * P, r1 * P)
+
+        def quantize_k(b):
+            quantize(k_codes[b], k_sc[b], k_grouped[b], 0, S)
+
+        def quantize_v(b):
+            quantize(v_codes[b], v_sc[b], v_grouped[b], 0, D)
+
+        def widen_v(b, block, engine):
+            for j in range(PACK):
+                lo = block * VBLOCK
+                codes = v_raw[b][:, j * D + lo : j * D + lo + VBLOCK].bitcast(FP8)
+                column = j * (D // VBLOCK) + block
+                mult = v_mult[:, b, column : column + 1]
+                dst = v_wide[b][:, j, lo : lo + VBLOCK]
+                if engine is nc.scalar:
+                    nc.scalar.activation(out=dst, in_=codes, func=ACT.Copy, scale=mult)
+                else:
+                    nc.vector.tensor_scalar(out=dst, in0=codes, scalar1=mult, scalar2=None, op0=ALU.mult)
+
+        def group_v(b, half, engine):
+            cols = slice(half * D // 2, (half + 1) * D // 2)
+            copy_on(
+                engine,
+                v_grouped[b][:, cols, :].rearrange("p (c i) t -> p c t i", i=4),
+                v_wide[b][:, :, cols].rearrange("p t (c i) -> p c t i", i=4),
             )
 
-        def widen_v(b, c, engine):
-            for f in range(4):
-                cols = slice(f * D + c * P, f * D + (c + 1) * P)
-                scale = v_sc[:, b, 4 * f + c : 4 * f + c + 1]
-                dst = v_wide[b][:, f, c * P : (c + 1) * P]
-                if engine is nc.scalar:
-                    nc.scalar.activation(out=dst, in_=v_raw[b][:, cols].bitcast(FP8), func=ACT.Copy, scale=scale)
-                else:
-                    nc.vector.tensor_scalar(
-                        out=dst, in0=v_raw[b][:, cols].bitcast(FP8), scalar1=scale, scalar2=None, op0=ALU.mult
-                    )
+        def spread_gains():
+            memory = ps_turn.tile([P, M], BF16, name="bank")
+            context = ps_out.tile([P, S], BF16, name="mixed")
+            for lo, dst in ((0, context[:]), (S, memory[:, 0:PART]), (S + PART, memory[:, PART:M])):
+                nc.tensor.matmul(dst, lhsT=ones[:], rhs=gain_rows[:, lo : lo + PART], start=True, stop=True)
+            nc.scalar.copy(out=gains[:, S:W], in_=memory[:])
+            nc.scalar.copy(out=gains[:, 0:S], in_=context[:])
 
-        def interleave_v(b, h, engine):
-            cols = slice(h * 256, (h + 1) * 256)
-            dst = v_grp[b][:, cols, :].rearrange("p (c i) f -> p c f i", i=4)
-            src = v_wide[b][:, :, cols].rearrange("p f (c i) -> p c f i", i=4)
-            if engine is nc.gpsimd:
-                nc.gpsimd.tensor_scalar(out=dst, in0=src, scalar1=1.0, scalar2=0.0, op0=ALU.mult, op1=ALU.add)
-            else:
-                copy_on(engine, dst, src)
-
-        LAST = NT - 1
-        SPLIT = (0, LAST)
-        banks, m3, nm, ex, z3, zs, fac, gained, probs, turned, grouped, pq = ({} for unused in range(12))
+        row = [{} for i in range(NT)]
 
         def score(i, c):
-            b, r = divmod(i, TPB)
-            sc = ps_score.tile([P, 512], F32, name="sc")
-            banks[i, c] = sc
+            b, r = divmod(i, ROW_TILES)
+            bank = ps_score.tile([P, PART], F32, name="scores")
+            row[i]["scores", c] = bank
             if c == 0:
-                rhs, rhs_scale = k_codes[b][:], k_plane[b][:]
+                keys, key_scales = k_codes[b][:], k_sc[b][:]
             else:
-                cols = slice((c - 1) * 512, c * 512)
-                rhs, rhs_scale = mk_codes[:, cols], mk_plane[:, cols]
+                cols = slice((c - 1) * PART, c * PART)
+                keys, key_scales = mk_codes[:, cols], mk_sc[:, cols]
             nc.tensor.matmul_mx(
-                out=sc[:],
+                out=bank[:],
                 lhsT=q_codes[b][:, r * P : (r + 1) * P].bitcast(FP8X4),
-                lhsT_scale=q_plane[b][:, r * P : (r + 1) * P],
-                rhs=rhs.bitcast(FP8X4),
-                rhs_scale=rhs_scale,
+                lhsT_scale=q_sc[b][:, r * P : (r + 1) * P],
+                rhs=keys.bitcast(FP8X4),
+                rhs_scale=key_scales,
                 start=True,
                 stop=True,
             )
 
         def row_max(i, c):
-            if i not in m3:
-                m3[i] = small.tile([P, 3], F32, name="m3_t")
-                nm[i] = small.tile([P, 3], F32, name="nm_t")
-            nc.vector.tensor_reduce(out=m3[i][:, c : c + 1], in_=banks[i, c][:], axis=AX.X, op=ALU.max)
+            if "max" not in row[i]:
+                row[i]["max"] = small.tile([P, 3], F32, name="maxima")
+                row[i]["shift"] = small.tile([P, 3], F32, name="shifts")
+            nc.vector.tensor_reduce(
+                out=row[i]["max"][:, c : c + 1], in_=row[i]["scores", c][:], axis=AX.X, op=ALU.max
+            )
+
+        def least(values, factor):
+            products = small.tile([P, 3], F32, name="products")
+            result = small.tile([P, 1], F32, name="least_of_three")
+            nc.vector.tensor_scalar(
+                out=products[:],
+                in0=values[:],
+                scalar1=factor,
+                scalar2=None,
+                op0=ALU.mult,
+                op1=ALU.min,
+                accum_out=result[:],
+            )
+            return result
+
+        def exponentials(i, c, shift):
+            if "exp" not in row[i]:
+                row[i]["exp"] = work.tile([P, W], F32, name="exp")
+                row[i]["sums"] = small.tile([P, 3], F32, name="sums")
+            nc.scalar.activation(
+                out=row[i]["exp"][:, c * PART : (c + 1) * PART],
+                in_=row[i]["scores", c][:],
+                func=ACT.Exp,
+                bias=shift,
+                scale=SCALE,
+                accum_out=row[i]["sums"][:, c : c + 1],
+            )
+
+        def joint_shift(i):
+            return least(row[i]["max"], -SCALE)
+
+        def joint_exponentials(i, shift):
+            for c in ORDER:
+                exponentials(i, c, shift[:])
+            copied = small.tile([P, 3], F32, name="copied")
+            row[i]["z"] = small.tile([P, 1], F32, name="z")
+            nc.scalar.activation(out=copied[:], in_=row[i]["sums"][:], func=ACT.Copy, accum_out=row[i]["z"][:])
 
         def own_shift(i, c):
             nc.vector.tensor_scalar(
-                out=nm[i][:, c : c + 1], in0=m3[i][:, c : c + 1], scalar1=-SCALE, scalar2=None, op0=ALU.mult
+                out=row[i]["shift"][:, c : c + 1],
+                in0=row[i]["max"][:, c : c + 1],
+                scalar1=-SCALE,
+                scalar2=None,
+                op0=ALU.mult,
             )
 
-        def join_shift(i, src):
-            j = small.tile([P, 1], F32, name="join")
-            scratch = small.tile([P, 3], F32, name="scratch")
+        def own_exponentials(i, c):
+            exponentials(i, c, row[i]["shift"][:, c : c + 1])
+
+        def part_weights(i):
+            joint = least(row[i]["shift"], 1.0)
+            row[i]["weight"] = small.tile([P, 3], F32, name="weights")
+            nc.scalar.activation(
+                out=row[i]["weight"][:], in_=row[i]["shift"][:], func=ACT.Exp, bias=joint[:], scale=-1.0
+            )
+
+        def weigh_sums(i):
+            row[i]["weighed"] = small.tile([P, 3], F32, name="weighed")
+            nc.vector.tensor_tensor(
+                out=row[i]["weighed"][:], in0=row[i]["sums"][:], in1=row[i]["weight"][:], op=ALU.mult
+            )
+
+        def add_weighed_sums(i):
+            row[i]["z"] = small.tile([P, 1], F32, name="z")
+            nc.vector.tensor_reduce(out=row[i]["z"][:], in_=row[i]["weighed"][:], axis=AX.X, op=ALU.add)
+
+        def invert_z(i):
+            row[i]["1/z"] = small.tile([P, 1], F32, name="inverse")
+            nc.vector.reciprocal(out=row[i]["1/z"][:], in_=row[i]["z"][:])
+
+        def part_factors(i):
+            row[i]["weight/z"] = small.tile([P, 3], F32, name="factors")
             nc.vector.tensor_scalar(
-                out=scratch[:], in0=src[:], scalar1=(1.0 if i in SPLIT else -SCALE), scalar2=None, op0=ALU.mult, op1=ALU.min, accum_out=j[:]
-            )
-            return j
-
-        def exponentials(i, c, bias):
-            if i not in ex:
-                ex[i] = work.tile([P, W], F32, name="ex_t")
-                z3[i] = small.tile([P, 3], F32, name="z3_t")
-            nc.scalar.activation(
-                out=ex[i][:, c * 512 : (c + 1) * 512],
-                in_=banks[i, c][:],
-                func=ACT.Exp,
-                bias=bias,
-                scale=SCALE,
-                accum_out=z3[i][:, c : c + 1],
+                out=row[i]["weight/z"][:],
+                in0=row[i]["weight"][:],
+                scalar1=row[i]["1/z"][:],
+                scalar2=None,
+                op0=ALU.mult,
             )
 
-        def z_join(i):
-            j = join_shift(i, nm[i])
-            fac[i] = small.tile([P, 3], F32, name="w3_t")
-            nc.scalar.activation(out=fac[i][:], in_=nm[i][:], func=ACT.Exp, bias=j[:], scale=-1.0)
-
-        def z_weigh(i):
-            zw = small.tile([P, 3], F32, name="zw_t")
-            nc.vector.tensor_tensor(out=zw[:], in0=z3[i][:], in1=fac[i][:], op=ALU.mult)
-            z3[i] = zw
-
-        def z_sum(i):
-            zs[i] = small.tile([P, 1], F32, name="zs_t")
-            if i in SPLIT:
-                nc.vector.tensor_reduce(out=zs[i][:], in_=z3[i][:], axis=AX.X, op=ALU.add)
-            else:
-                z_parts = small.tile([P, 3], F32, name="z_parts")
-                nc.scalar.activation(out=z_parts[:], in_=z3[i][:], func=ACT.Copy, accum_out=zs[i][:])
-
-        def z_inv(i):
-            inv = small.tile([P, 1], F32, name="inv")
-            nc.vector.reciprocal(out=inv[:], in_=zs[i][:])
-            zs[i] = inv
-
-        def z_factors(i):
-            if i in SPLIT:
-                f3 = small.tile([P, 3], F32, name="f3_t")
-                nc.vector.tensor_scalar(out=f3[:], in0=fac[i][:], scalar1=zs[i][:], scalar2=None, op0=ALU.mult)
-                fac[i] = [f3[:, c : c + 1] for c in range(3)]
-            else:
-                fac[i] = [zs[i][:]] * 3
-
-        def probs_tile(i):
-            if i not in probs:
-                probs[i] = work.tile([P, W], BF16, align_bytes=64, name="pg")
-
-        def gain_first(i, c):
-            e_g = work.tile([P, 512], F32, name="e_g")
-            cols = slice(c * 512, (c + 1) * 512)
-            nc.gpsimd.tensor_tensor(out=e_g[:], in0=ex[i][:, cols], in1=gains[:, cols], op=ALU.mult)
-            gained[i] = e_g
-
-        def factor_last(i, c):
-            probs_tile(i)
-            nc.scalar.activation(
-                out=probs[i][:, c * 512 : (c + 1) * 512], in_=gained[i][:], func=ACT.Copy, scale=fac[i][c]
-            )
-
-        def normalise(i, lo, hi):
-            probs_tile(i)
-            cols = slice(lo * 512, hi * 512)
+        def normalise(i, c0, c1):
+            if "gained" not in row[i]:
+                row[i]["gained"] = work.tile([P, W], BF16, align_bytes=64, name="gained")
+            cols = slice(c0 * PART, c1 * PART)
             nc.vector.scalar_tensor_tensor(
-                out=probs[i][:, cols], in0=ex[i][:, cols], scalar=fac[i][lo], in1=gains[:, cols], op0=ALU.mult, op1=ALU.mult
+                out=row[i]["gained"][:, cols],
+                in0=row[i]["exp"][:, cols],
+                scalar=row[i]["weight/z"][:, c0 : c0 + 1] if i in OWN_SHIFTS else row[i]["1/z"][:],
+                in1=gains[:, cols],
+                op0=ALU.mult,
+                op1=ALU.mult,
             )
 
-        def turn_probs(i, lo, hi):
-            words = probs[i][:].bitcast(F32)
-            bank = ps_turn.tile([P, hi - lo, 2, P], F32, name="bank")
-            turned[i, lo] = bank
-            for g in range(lo, hi):
-                for e in range(2):
-                    nc.tensor.transpose(bank[:, g - lo, e, :], words[:, 256 * g + e : 256 * (g + 1) : 2], ident[:])
+        def turn_gained(i, c0, c1):
+            bank = ps_turn.tile([P, c1 - c0, 2, P], F32, name="bank")
+            row[i]["turned", c0] = bank
+            turn(bank, row[i]["gained"][:].bitcast(F32), c0, c1 - c0)
 
-        def copy_probs(i, lo, hi, engine):
-            if i not in grouped:
-                grouped[i] = work.tile([P, 3 * P, 4], BF16, align_bytes=64, name="pg_grp")
-            dst = grouped[i][:].rearrange("p n f -> p (n f)").bitcast(F32).rearrange("p (a n e) -> p a n e", a=3, e=2)
-            copy_on(engine, dst[:, lo:hi], turned[i, lo][:].rearrange("p a e n -> p a n e"))
+        def group_gained(i, c0, c1, engine):
+            if "grouped" not in row[i]:
+                row[i]["grouped"] = work.tile([P, 3 * P, PACK], BF16, align_bytes=64, name="grouped")
+            group(engine, row[i]["grouped"][:, c0 * P : c1 * P, :], row[i]["turned", c0])
 
-        def quantize_probs(i, lo, hi):
-            if i not in pq:
-                codes = work.tile([P, 3 * P], U32, align_bytes=64, name="p_codes")
-                plane = work.tile([P, 3 * P], U8, align_bytes=64, name="p_plane")
-                pq[i] = (codes, plane)
-            codes, plane = pq[i]
-            quantize(codes, plane, grouped[i], lo * P, hi * P)
+        def quantize_gained(i, c0, c1):
+            if "codes" not in row[i]:
+                row[i]["codes"] = work.tile([P, 3 * P], U32, align_bytes=64, name="codes")
+                row[i]["scales"] = work.tile([P, 3 * P], U8, align_bytes=64, name="scales")
+            quantize(row[i]["codes"], row[i]["scales"], row[i]["grouped"], c0 * P, c1 * P)
 
-        def mix(i, o, g, first, last, lo=0, hi=D):
-            b = i // TPB
-            codes, plane = pq[i]
-            if g == 0:
-                rhs, rhs_scale = v_codes[b][:, lo:hi], v_plane[b][:, lo:hi]
-            elif g == 1:
-                rhs, rhs_scale = mv_codes[:, 0, lo:hi], mv_plane[:, lo:hi]
+        def mix_part(i, c, dst, lo, hi):
+            b = i // ROW_TILES
+            if c == 0:
+                values, value_scales = v_codes[b][:, lo:hi], v_sc[b][:, lo:hi]
             else:
-                rhs, rhs_scale = mv_codes[:, 1, lo:hi], mv_plane[4:P, lo:hi]
+                values, value_scales = mv_codes[:, c - 1, lo:hi], mv_sc[4 * (c - 1) : P, lo:hi]
+            rows = slice(c * P, (c + 1) * P)
             nc.tensor.matmul_mx(
-                out=o,
-                lhsT=codes[:, g * P : (g + 1) * P].bitcast(FP8X4),
-                lhsT_scale=plane[:, g * P : (g + 1) * P],
-                rhs=rhs.bitcast(FP8X4),
-                rhs_scale=rhs_scale,
-                start=first,
-                stop=last,
+                out=dst,
+                lhsT=row[i]["codes"][:, rows].bitcast(FP8X4),
+                lhsT_scale=row[i]["scales"][:, rows],
+                rhs=values.bitcast(FP8X4),
+                rhs_scale=value_scales,
+                start=(c == ORDER[0]),
+                stop=(c == ORDER[-1]),
             )
 
-        acc = {}
+        def mix(i, pool, name):
+            row[i]["mixed"] = pool.tile([P, D], F32, name=name)
+            for c in ORDER:
+                mix_part(i, c, row[i]["mixed"][:], 0, D)
 
-        def mix_tile(i):
-            if i == LAST - 1:
-                acc[i] = ps_score.tile([P, D], F32, name="sc")
-            else:
-                acc[i] = ps_out.tile([P, D], F32, name="o")
-            for n, g in enumerate((1, 2, 0)):
-                mix(i, acc[i][:], g, n == 0, n == 2)
+        def store(i, src, lo, hi, engine):
+            b, r = divmod(i, ROW_TILES)
+            result = results.tile([P, hi - lo], F32, name="result")
+            copy_on(engine, result[:], src)
+            nc.sync.dma_start(out=out[b, r * P : (r + 1) * P, lo:hi], in_=result[:])
 
-        def store(i, o, lo, hi, engine):
-            b, r = divmod(i, TPB)
-            res = results.tile([P, hi - lo], F32, name="res")
-            copy_on(engine, res[:], o)
-            nc.sync.dma_start(out=out[b, r * P : (r + 1) * P, lo:hi], in_=res[:])
+        def store_tile(i):
+            store(i, row[i]["mixed"][:], 0, D, nc.scalar)
 
-
-        turn_rows(q_raw[0], q_grp[0], 0, 1, nc.scalar)
-        quantize(q_codes[0], q_plane[0], q_grp[0], 0, P)
-        widen_v(0, 0, nc.vector)
-        widen_v(0, 1, nc.vector)
-        widen_v(0, 2, nc.scalar)
+        scalar, vector = nc.scalar, nc.vector
+        turn_rows(q_raw[0], q_grouped[0], 0, 1, scalar)
+        quantize_q(0, 0, 1)
+        widen_v(0, 0, vector)
+        widen_v(0, 3, scalar)
         score(0, 1)
         score(0, 2)
-        widen_v(0, 3, nc.vector)
-        interleave_v(0, 0, nc.vector)
+        widen_v(0, 1, vector)
+        widen_v(0, 2, vector)
+        group_v(0, 0, scalar)
         row_max(0, 1)
-        turn_rows(k_raw[0], k_grp[0], 0, 2, nc.scalar)
+        turn_rows(k_raw[0], k_grouped[0], 0, 2, scalar)
         row_max(0, 2)
         own_shift(0, 1)
         own_shift(0, 2)
-        turn_rows(k_raw[0], k_grp[0], 2, 2, nc.vector)
-        exponentials(0, 1, nm[0][:, 1:2])
-        turn_rows(q_raw[0], q_grp[0], 1, 2, nc.scalar)
-        quantize(k_codes[0], k_plane[0], k_grp[0], 0, S)
-        exponentials(0, 2, nm[0][:, 2:3])
+        turn_rows(k_raw[0], k_grouped[0], 2, 2, vector)
+        own_exponentials(0, 1)
+        turn_rows(q_raw[0], q_grouped[0], 1, 2, scalar)
+        quantize_k(0)
+        own_exponentials(0, 2)
         score(0, 0)
-        quantize(q_codes[0], q_plane[0], q_grp[0], P, 3 * P)
-        turn_rows(k_raw[1], k_grp[1], 2, 2, nc.scalar)
+        quantize_q(0, 1, 3)
+        turn_rows(k_raw[1], k_grouped[1], 2, 2, scalar)
+        group_v(0, 1, vector)
         row_max(0, 0)
         score(1, 1)
         score(1, 2)
         own_shift(0, 0)
         row_max(1, 1)
-        exponentials(0, 0, nm[0][:, 0:1])
-        z_join(0)
+        own_exponentials(0, 0)
+        part_weights(0)
         score(1, 0)
-        turn_rows(q_raw[0], q_grp[0], 3, 1, nc.scalar)
-        spread_m = ps_turn.tile([P, M], BF16, name="bank")
-        spread_c = ps_out.tile([P, S], BF16, name="o")
-        for lo, bank in ((0, spread_c[:]), (S, spread_m[:, 0:512]), (S + 512, spread_m[:, 512:1024])):
-            nc.tensor.matmul(bank, lhsT=ones[:], rhs=gain_rows[:, lo : lo + 512], start=True, stop=True)
-        nc.scalar.copy(out=gains[:, S:W], in_=spread_m[:])
-        nc.scalar.copy(out=gains[:, 0:S], in_=spread_c[:])
-        interleave_v(0, 1, nc.vector)
-        turn_rows(k_raw[1], k_grp[1], 0, 2, nc.scalar)
-        z_weigh(0)
+        turn_rows(q_raw[0], q_grouped[0], 3, 1, scalar)
+        spread_gains()
+        turn_rows(q_raw[1], q_grouped[1], 2, 2, scalar)
+
+        quantize_v(0)
+        weigh_sums(0)
         row_max(1, 2)
-        z_sum(0)
+        add_weighed_sums(0)
         row_max(1, 0)
-        z_inv(0)
-        quantize(v_codes[0], v_plane[0], v_grp[0], 0, D)
-        j = join_shift(1, m3[1])
-        z_factors(0)
-        for c in CHUNKS:
-            exponentials(1, c, j[:])
-        z_sum(1)
-        normalise(0, 1, 2)
-        normalise(0, 2, 3)
-        normalise(0, 0, 1)
-        turn_rows(q_raw[1], q_grp[1], 0, 2, nc.scalar)
-        turn_rows(q_raw[1], q_grp[1], 2, 2, nc.scalar)
-        quantize(q_codes[0], q_plane[0], q_grp[0], 3 * P, S)
-        for c in CHUNKS:
+        invert_z(0)
+        shift = joint_shift(1)
+        part_factors(0)
+        joint_exponentials(1, shift)
+        for c in ORDER:
+            normalise(0, c, c + 1)
+        turn_rows(k_raw[1], k_grouped[1], 0, 2, scalar)
+        turn_rows(q_raw[1], q_grouped[1], 0, 2, scalar)
+        for c in ORDER:
             score(2, c)
-        turn_probs(0, 1, 3)
-        turn_probs(0, 0, 1)
-        copy_probs(0, 1, 3, nc.scalar)
-        row_max(2, 1)
-        copy_probs(0, 0, 1, nc.scalar)
-        row_max(2, 2)
-        z_inv(1)
-        row_max(2, 0)
-        z_factors(1)
-        quantize(k_codes[1], k_plane[1], k_grp[1], 0, S)
-        j = join_shift(2, m3[2])
-        for c in CHUNKS:
-            exponentials(2, c, j[:])
-        z_sum(2)
-        normalise(1, 1, 2)
-        normalise(1, 2, 3)
-        normalise(1, 0, 1)
-        quantize_probs(0, 1, 3)
-        quantize_probs(0, 0, 1)
-        widen_v(1, 0, nc.scalar)
-        for c in CHUNKS:
-            score(3, c)
-        turn_probs(1, 1, 3)
-        turn_probs(1, 0, 1)
-        mix_tile(0)
-        copy_probs(1, 1, 3, nc.scalar)
-        row_max(3, 1)
-        copy_probs(1, 0, 1, nc.scalar)
-        row_max(3, 2)
-        z_inv(2)
-        row_max(3, 0)
-        z_factors(2)
-        store(0, acc[0][:], 0, D, nc.scalar)
-        quantize(q_codes[1], q_plane[1], q_grp[1], 0 * P, 2 * P)
-        j = join_shift(3, m3[3])
-        for c in CHUNKS:
-            exponentials(3, c, j[:])
-        z_sum(3)
-        normalise(2, 1, 2)
-        normalise(2, 2, 3)
-        normalise(2, 0, 1)
-        quantize_probs(1, 1, 3)
-        quantize_probs(1, 0, 1)
-        for c in CHUNKS:
-            score(4, c)
-        turn_probs(2, 1, 3)
-        turn_probs(2, 0, 1)
-        mix_tile(1)
-        widen_v(1, 2, nc.scalar)
-        copy_probs(2, 1, 3, nc.scalar)
-        row_max(4, 1)
-        copy_probs(2, 0, 1, nc.scalar)
-        row_max(4, 2)
-        z_inv(3)
-        row_max(4, 0)
-        z_factors(3)
-        store(1, acc[1][:], 0, D, nc.scalar)
-        widen_v(1, 1, nc.vector)
-        j = join_shift(4, m3[4])
-        for c in CHUNKS:
-            exponentials(4, c, j[:])
-        z_sum(4)
-        normalise(3, 1, 2)
-        normalise(3, 2, 3)
-        normalise(3, 0, 1)
-        quantize_probs(2, 1, 3)
-        quantize_probs(2, 0, 1)
-        for c in CHUNKS:
-            score(5, c)
-        turn_probs(3, 1, 3)
-        turn_probs(3, 0, 1)
-        mix_tile(2)
-        widen_v(1, 3, nc.scalar)
-        quantize(q_codes[1], q_plane[1], q_grp[1], 2 * P, 4 * P)
-        copy_probs(3, 1, 3, nc.scalar)
-        row_max(5, 1)
-        copy_probs(3, 0, 1, nc.scalar)
-        row_max(5, 2)
-        z_inv(4)
-        row_max(5, 0)
-        z_factors(4)
-        store(2, acc[2][:], 0, D, nc.scalar)
-        j = join_shift(5, m3[5])
-        for c in CHUNKS:
-            exponentials(5, c, j[:])
-        z_sum(5)
-        normalise(4, 1, 2)
-        normalise(4, 2, 3)
-        normalise(4, 0, 1)
-        quantize_probs(3, 1, 3)
-        quantize_probs(3, 0, 1)
-        interleave_v(1, 0, nc.scalar)
-        for c in CHUNKS:
-            score(6, c)
-        turn_probs(4, 1, 3)
-        turn_probs(4, 0, 1)
-        mix_tile(3)
-        copy_probs(4, 1, 3, nc.scalar)
-        row_max(6, 1)
-        copy_probs(4, 0, 1, nc.scalar)
-        row_max(6, 2)
-        z_inv(5)
-        row_max(6, 0)
-        z_factors(5)
-        store(3, acc[3][:], 0, D, nc.scalar)
-        interleave_v(1, 1, nc.vector)
-        j = join_shift(6, m3[6])
-        for c in CHUNKS:
-            exponentials(6, c, j[:])
-        z_sum(6)
-        normalise(5, 1, 2)
-        normalise(5, 2, 3)
-        normalise(5, 0, 1)
-        quantize_probs(4, 1, 3)
-        quantize_probs(4, 0, 1)
-        quantize(v_codes[1], v_plane[1], v_grp[1], 0, D)
-        for c in CHUNKS:
-            score(7, c)
-        turn_probs(5, 1, 3)
-        turn_probs(5, 0, 1)
-        mix_tile(4)
-        copy_probs(5, 1, 3, nc.scalar)
-        row_max(7, 1)
-        copy_probs(5, 0, 1, nc.scalar)
-        own_shift(7, 1)
-        exponentials(7, 1, nm[7][:, 1:2])
-        row_max(7, 2)
-        z_inv(6)
-        own_shift(7, 2)
-        exponentials(7, 2, nm[7][:, 2:3])
-        row_max(7, 0)
-        z_factors(6)
-        own_shift(7, 0)
-        exponentials(7, 0, nm[7][:, 0:1])
-        z_join(7)
-        store(4, acc[4][:], 0, D, nc.scalar)
-        normalise(6, 1, 2)
-        normalise(6, 2, 3)
-        normalise(6, 0, 1)
-        z_weigh(7)
-        quantize_probs(5, 1, 3)
-        z_sum(7)
-        quantize_probs(5, 0, 1)
-        turn_probs(6, 1, 3)
-        turn_probs(6, 0, 1)
-        mix_tile(5)
-        copy_probs(LAST - 1, 1, 3, nc.scalar)
-        z_inv(LAST)
-        z_factors(LAST)
-        copy_probs(LAST - 1, 0, 1, nc.scalar)
-        normalise(LAST, 1, 2)
-        normalise(LAST, 2, 3)
-        normalise(LAST, 0, 1)
-        quantize_probs(LAST - 1, 1, 3)
-        quantize_probs(LAST - 1, 0, 1)
-        turn_probs(LAST, 1, 2)
-        turn_probs(LAST, 2, 3)
-        turn_probs(LAST, 0, 1)
-        mix_tile(LAST - 1)
-        copy_probs(LAST, 1, 2, nc.scalar)
-        copy_probs(LAST, 2, 3, nc.scalar)
-        quantize_probs(LAST, 1, 2)
-        quantize_probs(LAST, 2, 3)
-        copy_probs(LAST, 0, 1, nc.vector)
-        store(LAST - 2, acc[LAST - 2][:], 0, D, nc.scalar)
-        quantize_probs(LAST, 0, 1)
-        left = ps_score.tile([P, 512], F32, name="sc")
-        right = ps_score.tile([P, 512], F32, name="sc")
-        for n, g in enumerate((1, 2, 0)):
-            mix(LAST, left[:, 0:256], g, n == 0, n == 2, 0, 256)
-            mix(LAST, right[:, 0:256], g, n == 0, n == 2, 256, 512)
-        store(LAST - 1, acc[LAST - 1][:], 0, D, nc.scalar)
-        store(LAST, left[:, 0:256], 0, 256, nc.scalar)
-        store(LAST, right[:, 0:256], 256, 512, nc.vector)
+        turn_gained(0, 1, 3)
+        turn_gained(0, 0, 1)
+
+        side_work = {
+            (2, "shift"): [lambda: quantize_q(0, 3, 4)],
+            (2, "end"): [lambda: quantize_q(1, 0, 2)],
+            (3, "start"): [lambda: widen_v(1, 0, scalar)],
+            (3, "shift"): [lambda: quantize_k(1)],
+            (4, "start"): [lambda: widen_v(1, 2, scalar)],
+            (4, "shift"): [lambda: quantize_q(1, 2, 4)],
+            (4, "end"): [lambda: widen_v(1, 3, scalar)],
+            (5, "shift"): [lambda: widen_v(1, 1, vector)],
+            (5, "end"): [lambda: group_v(1, 0, scalar)],
+            (6, "shift"): [lambda: group_v(1, 1, vector)],
+            (6, "end"): [lambda: quantize_v(1)],
+        }
+
+        def side(s, place):
+            for entry in side_work.get((s, place), ()):
+                entry()
+
+        for s in range(2, NT):
+            side(s, "start")
+            group_gained(s - 2, 1, 3, scalar)
+            row_max(s, 1)
+            group_gained(s - 2, 0, 1, scalar)
+            if s == LAST:
+                own_shift(s, 1)
+                own_exponentials(s, 1)
+            row_max(s, 2)
+            invert_z(s - 1)
+            if s == LAST:
+                own_shift(s, 2)
+                own_exponentials(s, 2)
+            row_max(s, 0)
+            if 3 <= s < LAST:
+                store_tile(s - 3)
+            side(s, "shift")
+            if s < LAST:
+                joint_exponentials(s, joint_shift(s))
+            else:
+                own_shift(s, 0)
+                own_exponentials(s, 0)
+                part_weights(s)
+                store_tile(s - 3)
+            normalise(s - 1, 1, 3)
+            normalise(s - 1, 0, 1)
+            if s == LAST:
+                weigh_sums(s)
+            quantize_gained(s - 2, 1, 3)
+            if s == LAST:
+                add_weighed_sums(s)
+            quantize_gained(s - 2, 0, 1)
+            side(s, "end")
+            if s < LAST:
+                for c in ORDER:
+                    score(s + 1, c)
+            turn_gained(s - 1, 1, 3)
+            turn_gained(s - 1, 0, 1)
+            mix(s - 2, ps_out, "mixed")
+
+        group_gained(LAST - 1, 1, 3, scalar)
+        invert_z(LAST)
+        part_factors(LAST)
+        group_gained(LAST - 1, 0, 1, scalar)
+        for c in ORDER:
+            normalise(LAST, c, c + 1)
+        quantize_gained(LAST - 1, 1, 3)
+        quantize_gained(LAST - 1, 0, 1)
+        for c in ORDER:
+            turn_gained(LAST, c, c + 1)
+        mix(LAST - 1, ps_score, "scores")
+        group_gained(LAST, 1, 2, scalar)
+        group_gained(LAST, 2, 3, scalar)
+        quantize_gained(LAST, 1, 2)
+        quantize_gained(LAST, 2, 3)
+        group_gained(LAST, 0, 1, vector)
+        store_tile(LAST - 2)
+        quantize_gained(LAST, 0, 1)
+        left = ps_score.tile([P, PART], F32, name="scores")
+        right = ps_score.tile([P, PART], F32, name="scores")
+        half = D // 2
+        for c in ORDER:
+            mix_part(LAST, c, left[:, 0:half], 0, half)
+            mix_part(LAST, c, right[:, 0:half], half, D)
+        store_tile(LAST - 1)
+        store(LAST, left[:, 0:half], 0, half, scalar)
+        store(LAST, right[:, 0:half], half, D, vector)

import math
from contextlib import ExitStack

import concourse.mybir as mybir
from concourse.masks import make_identity

B, S, M, D = 2, 512, 1024, 512
FLOPS = 2 * 2 * B * S * (S + M) * D

F32 = mybir.dt.float32
BF16 = mybir.dt.bfloat16
I32 = mybir.dt.int32
U32 = mybir.dt.uint32
U8 = mybir.dt.uint8
FP8 = mybir.dt.float8_e4m3fn
FP8X4 = mybir.dt.float8_e4m3fn_x4
ALU = mybir.AluOpType
ACT = mybir.ActivationFunctionType
AX = mybir.AxisListType

P = 128
PACK = 4
PART = 512
W = S + M
ORDER = (1, 2, 0)
ROW_TILES = S // P
NT = B * ROW_TILES
LAST = NT - 1
VBLOCK = 128
SCALE = 1.0 / math.sqrt(D)
OWN_SHIFTS = (0, LAST)


def tile_persistentmemoryallattentionsignedgains_d1p_kernel(
    tc, q, k, mk_words, mk_scales, v_bytes, v_scale, mv_words, mv_scales, t, u, out
):
    nc = tc.nc
    with ExitStack() as ctx:
        const = ctx.enter_context(tc.tile_pool(name="const", bufs=1))
        work = ctx.enter_context(tc.tile_pool(name="work", bufs=4))
        results = ctx.enter_context(tc.tile_pool(name="results", bufs=6))
        small = ctx.enter_context(tc.tile_pool(name="small", bufs=6))
        ps_score = ctx.enter_context(tc.psum_pool(name="ps_score", bufs=4))
        ps_turn = ctx.enter_context(tc.psum_pool(name="ps_turn", bufs=3))
        ps_out = ctx.enter_context(tc.psum_pool(name="ps_out", bufs=1))
        ctx.enter_context(tc.manual_schedule())

        gain_rows = const.tile([P, W], BF16, name="gain_rows")
        nc.vector.memset(gain_rows[:].bitcast(I32), 0)
        mk_sc = const.tile([P, M], U8, align_bytes=64, name="mk_sc")
        mv_sc = const.tile([P, D], U8, align_bytes=64, name="mv_sc")
        nc.vector.memset(mk_sc[:].bitcast(I32), 0)
        nc.vector.memset(mv_sc[:].bitcast(I32), 0)
        zeros = const.tile([P, P], BF16, name="zeros")
        nc.vector.memset(zeros[:], 0.0)
        ident = const.tile([P, P], F32, name="ident")
        make_identity(nc, ident[:])

        q_raw = [const.tile([P, ROW_TILES, D], BF16, name="q_raw%d" % b) for b in range(B)]
        k_raw = [const.tile([P, ROW_TILES, D], BF16, name="k_raw%d" % b) for b in range(B)]
        v_raw = [const.tile([P, PACK * D], U8, name="v_raw%d" % b) for b in range(B)]
        mk_codes = const.tile([P, M], I32, align_bytes=64, name="mk_codes")
        mv_codes = const.tile([P, 2, D], I32, align_bytes=64, name="mv_codes")
        v_mult = const.tile([P, B, PACK * (D // VBLOCK)], F32, name="v_mult")
        gains = const.tile([P, W], BF16, name="gains")
        ones = const.tile([P, P], BF16, name="ones")
        nc.scalar.dma_start(out=gain_rows[0:1, 0:S], in_=t.rearrange("(o n) -> o n", o=1))
        nc.scalar.dma_start(out=gain_rows[0:1, S:W], in_=u.rearrange("(o n) -> o n", o=1))
        nc.scalar.activation(out=ones[:], in_=zeros[:], func=ACT.Exp)

        def load_rows(dst, src, lo, hi):
            nc.sync.dma_start(out=dst[:, lo:hi, :], in_=src.rearrange("(r p) d -> p r d", p=P)[:, lo:hi, :])

        def load_v(b):
            nc.sync.dma_start(out=v_raw[b][:], in_=v_bytes[b].rearrange("(p t) n -> p (t n)", t=PACK))

        def load_scale_rows(dst, first, rows):
            for quarter in range(4):
                nc.sync.dma_start(
                    out=dst[32 * quarter + first : 32 * quarter + first + 4, :].bitcast(I32),
                    in_=rows[4 * quarter : 4 * quarter + 4, :].bitcast(I32),
                )

        load_rows(q_raw[0], q[0], 0, 1)
        nc.sync.dma_start(out=v_mult[:], in_=v_scale.rearrange("b (p t) c -> p b (t c)", t=PACK))
        load_v(0)
        load_scale_rows(mk_sc, 0, mk_scales[0])
        for h in range(2):
            cols = slice(h * PART, (h + 1) * PART)
            nc.sync.dma_start(
                out=mk_codes[:, cols], in_=mk_words[0, :, cols, :].rearrange("p n t -> p (n t)").bitcast(I32)
            )
        load_rows(k_raw[0], k[0], 0, 2)
        load_rows(k_raw[0], k[0], 2, 4)
        load_rows(q_raw[0], q[0], 1, 4)
        load_v(1)
        load_rows(k_raw[1], k[1], 0, 4)
        for g in range(2):
            nc.sync.dma_start(out=mv_codes[:, g, :], in_=mv_words[g].rearrange("p n t -> p (n t)").bitcast(I32))
        for g in range(2):
            load_scale_rows(mv_sc, 4 * g, mv_scales[g])
        load_rows(q_raw[1], q[1], 0, 4)

        q_codes = [const.tile([P, S], U32, align_bytes=64, name="q_codes%d" % b) for b in range(B)]
        q_sc = [const.tile([P, S], U8, align_bytes=64, name="q_sc%d" % b) for b in range(B)]
        k_codes = [const.tile([P, S], U32, align_bytes=64, name="k_codes%d" % b) for b in range(B)]
        k_sc = [const.tile([P, S], U8, align_bytes=64, name="k_sc%d" % b) for b in range(B)]
        v_codes = [const.tile([P, D], U32, align_bytes=64, name="v_codes%d" % b) for b in range(B)]
        v_sc = [const.tile([P, D], U8, align_bytes=64, name="v_sc%d" % b) for b in range(B)]
        q_grouped = [const.tile([P, S, PACK], BF16, align_bytes=64, name="q_grouped%d" % b) for b in range(B)]
        k_grouped = [const.tile([P, S, PACK], BF16, align_bytes=64, name="k_grouped%d" % b) for b in range(B)]
        v_wide = [const.tile([P, PACK, D], BF16, align_bytes=64, name="v_wide%d" % b) for b in range(B)]
        v_grouped = [const.tile([P, D, PACK], BF16, align_bytes=64, name="v_grouped%d" % b) for b in range(B)]

        def copy_on(engine, dst, src):
            if engine is nc.scalar:
                nc.scalar.copy(out=dst, in_=src)
            else:
                nc.vector.tensor_copy(out=dst, in_=src)

        def quantize(codes, scales, grouped, lo, hi):
            nc.vector.quantize_mx(
                out=codes[:, lo:hi].bitcast(FP8X4),
                scales=scales[:, lo:hi],
                in_=grouped[:, lo:hi, :].rearrange("p n t -> p (n t)"),
            )

        def turn(bank, words, first, count):
            run = PART // 2
            for a in range(count):
                for e in range(2):
                    lo = (first + a) * run
                    nc.tensor.transpose(bank[:, a, e, :], words[:, lo + e : lo + run : 2], ident[:])

        def group(engine, dst, bank):
            count = bank.shape[1]
            words = dst.rearrange("p n t -> p (n t)").bitcast(F32)
            copy_on(
                engine,
                words.rearrange("p (a n e) -> p a n e", a=count, e=2),
                bank[:].rearrange("p a e n -> p a n e"),
            )

        def turn_rows(raw, grouped, r0, count, engine):
            bank = ps_turn.tile([P, count, 2, P], F32, name="bank")
            turn(bank, raw[:].rearrange("p r d -> p (r d)").bitcast(F32), r0, count)
            group(engine, grouped[:, r0 * P : (r0 + count) * P, :], bank)

        def quantize_q(b, r0, r1):
            quantize(q_codes[b], q_sc[b], q_grouped[b], r0 * P, r1 * P)

        def quantize_k(b):
            quantize(k_codes[b], k_sc[b], k_grouped[b], 0, S)

        def quantize_v(b):
            quantize(v_codes[b], v_sc[b], v_grouped[b], 0, D)

        def widen_v(b, block, engine):
            for j in range(PACK):
                lo = block * VBLOCK
                codes = v_raw[b][:, j * D + lo : j * D + lo + VBLOCK].bitcast(FP8)
                column = j * (D // VBLOCK) + block
                mult = v_mult[:, b, column : column + 1]
                dst = v_wide[b][:, j, lo : lo + VBLOCK]
                if engine is nc.scalar:
                    nc.scalar.activation(out=dst, in_=codes, func=ACT.Copy, scale=mult)
                else:
                    nc.vector.tensor_scalar(out=dst, in0=codes, scalar1=mult, scalar2=None, op0=ALU.mult)

        def group_v(b, half, engine):
            cols = slice(half * D // 2, (half + 1) * D // 2)
            copy_on(
                engine,
                v_grouped[b][:, cols, :].rearrange("p (c i) t -> p c t i", i=4),
                v_wide[b][:, :, cols].rearrange("p t (c i) -> p c t i", i=4),
            )

        def spread_gains():
            memory = ps_turn.tile([P, M], BF16, name="bank")
            context = ps_out.tile([P, S], BF16, name="mixed")
            for lo, dst in ((0, context[:]), (S, memory[:, 0:PART]), (S + PART, memory[:, PART:M])):
                nc.tensor.matmul(dst, lhsT=ones[:], rhs=gain_rows[:, lo : lo + PART], start=True, stop=True)
            nc.scalar.copy(out=gains[:, S:W], in_=memory[:])
            nc.scalar.copy(out=gains[:, 0:S], in_=context[:])

        row = [{} for i in range(NT)]

        def score(i, c):
            b, r = divmod(i, ROW_TILES)
            bank = ps_score.tile([P, PART], F32, name="scores")
            row[i]["scores", c] = bank
            if c == 0:
                keys, key_scales = k_codes[b][:], k_sc[b][:]
            else:
                cols = slice((c - 1) * PART, c * PART)
                keys, key_scales = mk_codes[:, cols], mk_sc[:, cols]
            nc.tensor.matmul_mx(
                out=bank[:],
                lhsT=q_codes[b][:, r * P : (r + 1) * P].bitcast(FP8X4),
                lhsT_scale=q_sc[b][:, r * P : (r + 1) * P],
                rhs=keys.bitcast(FP8X4),
                rhs_scale=key_scales,
                start=True,
                stop=True,
            )

        def row_max(i, c):
            if "max" not in row[i]:
                row[i]["max"] = small.tile([P, 3], F32, name="maxima")
                row[i]["shift"] = small.tile([P, 3], F32, name="shifts")
            nc.vector.tensor_reduce(
                out=row[i]["max"][:, c : c + 1], in_=row[i]["scores", c][:], axis=AX.X, op=ALU.max
            )

        def least(values, factor):
            products = small.tile([P, 3], F32, name="products")
            result = small.tile([P, 1], F32, name="least_of_three")
            nc.vector.tensor_scalar(
                out=products[:],
                in0=values[:],
                scalar1=factor,
                scalar2=None,
                op0=ALU.mult,
                op1=ALU.min,
                accum_out=result[:],
            )
            return result

        def exponentials(i, c, shift):
            if "exp" not in row[i]:
                row[i]["exp"] = work.tile([P, W], F32, name="exp")
                row[i]["sums"] = small.tile([P, 3], F32, name="sums")
            nc.scalar.activation(
                out=row[i]["exp"][:, c * PART : (c + 1) * PART],
                in_=row[i]["scores", c][:],
                func=ACT.Exp,
                bias=shift,
                scale=SCALE,
                accum_out=row[i]["sums"][:, c : c + 1],
            )

        def joint_shift(i):
            return least(row[i]["max"], -SCALE)

        def joint_exponentials(i, shift):
            for c in ORDER:
                exponentials(i, c, shift[:])
            copied = small.tile([P, 3], F32, name="copied")
            row[i]["z"] = small.tile([P, 1], F32, name="z")
            nc.scalar.activation(out=copied[:], in_=row[i]["sums"][:], func=ACT.Copy, accum_out=row[i]["z"][:])

        def own_shift(i, c):
            nc.vector.tensor_scalar(
                out=row[i]["shift"][:, c : c + 1],
                in0=row[i]["max"][:, c : c + 1],
                scalar1=-SCALE,
                scalar2=None,
                op0=ALU.mult,
            )

        def own_exponentials(i, c):
            exponentials(i, c, row[i]["shift"][:, c : c + 1])

        def part_weights(i):
            joint = least(row[i]["shift"], 1.0)
            row[i]["weight"] = small.tile([P, 3], F32, name="weights")
            nc.scalar.activation(
                out=row[i]["weight"][:], in_=row[i]["shift"][:], func=ACT.Exp, bias=joint[:], scale=-1.0
            )

        def weigh_sums(i):
            row[i]["weighed"] = small.tile([P, 3], F32, name="weighed")
            nc.vector.tensor_tensor(
                out=row[i]["weighed"][:], in0=row[i]["sums"][:], in1=row[i]["weight"][:], op=ALU.mult
            )

        def add_weighed_sums(i):
            row[i]["z"] = small.tile([P, 1], F32, name="z")
            nc.vector.tensor_reduce(out=row[i]["z"][:], in_=row[i]["weighed"][:], axis=AX.X, op=ALU.add)

        def invert_z(i):
            row[i]["1/z"] = small.tile([P, 1], F32, name="inverse")
            nc.vector.reciprocal(out=row[i]["1/z"][:], in_=row[i]["z"][:])

        def part_factors(i):
            row[i]["weight/z"] = small.tile([P, 3], F32, name="factors")
            nc.vector.tensor_scalar(
                out=row[i]["weight/z"][:],
                in0=row[i]["weight"][:],
                scalar1=row[i]["1/z"][:],
                scalar2=None,
                op0=ALU.mult,
            )

        def normalise(i, c0, c1):
            if "gained" not in row[i]:
                row[i]["gained"] = work.tile([P, W], BF16, align_bytes=64, name="gained")
            cols = slice(c0 * PART, c1 * PART)
            nc.vector.scalar_tensor_tensor(
                out=row[i]["gained"][:, cols],
                in0=row[i]["exp"][:, cols],
                scalar=row[i]["weight/z"][:, c0 : c0 + 1] if i in OWN_SHIFTS else row[i]["1/z"][:],
                in1=gains[:, cols],
                op0=ALU.mult,
                op1=ALU.mult,
            )

        def turn_gained(i, c0, c1):
            bank = ps_turn.tile([P, c1 - c0, 2, P], F32, name="bank")
            row[i]["turned", c0] = bank
            turn(bank, row[i]["gained"][:].bitcast(F32), c0, c1 - c0)

        def group_gained(i, c0, c1, engine):
            if "grouped" not in row[i]:
                row[i]["grouped"] = work.tile([P, 3 * P, PACK], BF16, align_bytes=64, name="grouped")
            group(engine, row[i]["grouped"][:, c0 * P : c1 * P, :], row[i]["turned", c0])

        def quantize_gained(i, c0, c1):
            if "codes" not in row[i]:
                row[i]["codes"] = work.tile([P, 3 * P], U32, align_bytes=64, name="codes")
                row[i]["scales"] = work.tile([P, 3 * P], U8, align_bytes=64, name="scales")
            quantize(row[i]["codes"], row[i]["scales"], row[i]["grouped"], c0 * P, c1 * P)

        def mix_part(i, c, dst, lo, hi):
            b = i // ROW_TILES
            if c == 0:
                values, value_scales = v_codes[b][:, lo:hi], v_sc[b][:, lo:hi]
            else:
                values, value_scales = mv_codes[:, c - 1, lo:hi], mv_sc[4 * (c - 1) : P, lo:hi]
            rows = slice(c * P, (c + 1) * P)
            nc.tensor.matmul_mx(
                out=dst,
                lhsT=row[i]["codes"][:, rows].bitcast(FP8X4),
                lhsT_scale=row[i]["scales"][:, rows],
                rhs=values.bitcast(FP8X4),
                rhs_scale=value_scales,
                start=(c == ORDER[0]),
                stop=(c == ORDER[-1]),
            )

        def mix(i, pool, name):
            row[i]["mixed"] = pool.tile([P, D], F32, name=name)
            for c in ORDER:
                mix_part(i, c, row[i]["mixed"][:], 0, D)

        def store(i, src, lo, hi, engine):
            b, r = divmod(i, ROW_TILES)
            result = results.tile([P, hi - lo], F32, name="result")
            copy_on(engine, result[:], src)
            nc.sync.dma_start(out=out[b, r * P : (r + 1) * P, lo:hi], in_=result[:])

        def store_tile(i):
            store(i, row[i]["mixed"][:], 0, D, nc.scalar)

        scalar, vector = nc.scalar, nc.vector
        turn_rows(q_raw[0], q_grouped[0], 0, 1, scalar)
        quantize_q(0, 0, 1)
        widen_v(0, 0, vector)
        widen_v(0, 3, scalar)
        score(0, 1)
        score(0, 2)
        widen_v(0, 1, vector)
        widen_v(0, 2, vector)
        group_v(0, 0, scalar)
        row_max(0, 1)
        turn_rows(k_raw[0], k_grouped[0], 0, 2, scalar)
        row_max(0, 2)
        own_shift(0, 1)
        own_shift(0, 2)
        turn_rows(k_raw[0], k_grouped[0], 2, 2, vector)
        own_exponentials(0, 1)
        turn_rows(q_raw[0], q_grouped[0], 1, 2, scalar)
        quantize_k(0)
        own_exponentials(0, 2)
        score(0, 0)
        quantize_q(0, 1, 3)
        turn_rows(k_raw[1], k_grouped[1], 2, 2, scalar)
        group_v(0, 1, vector)
        row_max(0, 0)
        score(1, 1)
        score(1, 2)
        own_shift(0, 0)
        row_max(1, 1)
        own_exponentials(0, 0)
        part_weights(0)
        score(1, 0)
        turn_rows(q_raw[0], q_grouped[0], 3, 1, scalar)
        spread_gains()
        turn_rows(q_raw[1], q_grouped[1], 2, 2, scalar)

        quantize_v(0)
        weigh_sums(0)
        row_max(1, 2)
        add_weighed_sums(0)
        row_max(1, 0)
        invert_z(0)
        shift = joint_shift(1)
        part_factors(0)
        joint_exponentials(1, shift)
        for c in ORDER:
            normalise(0, c, c + 1)
        turn_rows(k_raw[1], k_grouped[1], 0, 2, scalar)
        turn_rows(q_raw[1], q_grouped[1], 0, 2, scalar)
        for c in ORDER:
            score(2, c)
        turn_gained(0, 1, 3)
        turn_gained(0, 0, 1)

        side_work = {
            (2, "shift"): [lambda: quantize_q(0, 3, 4)],
            (2, "end"): [lambda: quantize_q(1, 0, 2)],
            (3, "start"): [lambda: widen_v(1, 0, scalar)],
            (3, "shift"): [lambda: quantize_k(1)],
            (4, "start"): [lambda: widen_v(1, 2, scalar)],
            (4, "shift"): [lambda: quantize_q(1, 2, 4)],
            (4, "end"): [lambda: widen_v(1, 3, scalar)],
            (5, "shift"): [lambda: widen_v(1, 1, vector)],
            (5, "end"): [lambda: group_v(1, 0, scalar)],
            (6, "shift"): [lambda: group_v(1, 1, vector)],
            (6, "end"): [lambda: quantize_v(1)],
        }

        def side(s, place):
            for entry in side_work.get((s, place), ()):
                entry()

        for s in range(2, NT):
            side(s, "start")
            group_gained(s - 2, 1, 3, scalar)
            row_max(s, 1)
            group_gained(s - 2, 0, 1, scalar)
            if s == LAST:
                own_shift(s, 1)
                own_exponentials(s, 1)
            row_max(s, 2)
            invert_z(s - 1)
            if s == LAST:
                own_shift(s, 2)
                own_exponentials(s, 2)
            row_max(s, 0)
            if 3 <= s < LAST:
                store_tile(s - 3)
            side(s, "shift")
            if s < LAST:
                joint_exponentials(s, joint_shift(s))
            else:
                own_shift(s, 0)
                own_exponentials(s, 0)
                part_weights(s)
                store_tile(s - 3)
            normalise(s - 1, 1, 3)
            normalise(s - 1, 0, 1)
            if s == LAST:
                weigh_sums(s)
            quantize_gained(s - 2, 1, 3)
            if s == LAST:
                add_weighed_sums(s)
            quantize_gained(s - 2, 0, 1)
            side(s, "end")
            if s < LAST:
                for c in ORDER:
                    score(s + 1, c)
            turn_gained(s - 1, 1, 3)
            turn_gained(s - 1, 0, 1)
            mix(s - 2, ps_out, "mixed")

        group_gained(LAST - 1, 1, 3, scalar)
        invert_z(LAST)
        part_factors(LAST)
        group_gained(LAST - 1, 0, 1, scalar)
        for c in ORDER:
            normalise(LAST, c, c + 1)
        quantize_gained(LAST - 1, 1, 3)
        quantize_gained(LAST - 1, 0, 1)
        for c in ORDER:
            turn_gained(LAST, c, c + 1)
        mix(LAST - 1, ps_score, "scores")
        group_gained(LAST, 1, 2, scalar)
        group_gained(LAST, 2, 3, scalar)
        quantize_gained(LAST, 1, 2)
        quantize_gained(LAST, 2, 3)
        group_gained(LAST, 0, 1, vector)
        store_tile(LAST - 2)
        quantize_gained(LAST, 0, 1)
        left = ps_score.tile([P, PART], F32, name="scores")
        right = ps_score.tile([P, PART], F32, name="scores")
        half = D // 2
        for c in ORDER:
            mix_part(LAST, c, left[:, 0:half], 0, half)
            mix_part(LAST, c, right[:, 0:half], half, D)
        store_tile(LAST - 1)
        store(LAST, left[:, 0:half], 0, half, scalar)
        store(LAST, right[:, 0:half], half, D, vector)
